import numpy as np
import ml_dtypes


def mxq(x, axis, fmt="e4m3"):
    dtype, down = {"e4m3": (ml_dtypes.float8_e4m3fn, 7), "e5m2": (ml_dtypes.float8_e5m2, 14)}[fmt]
    v = np.moveaxis(np.asarray(x, np.float32).astype(ml_dtypes.bfloat16).astype(np.float64), axis, -1)
    blocks = v.reshape(v.shape[:-1] + (-1, 32))
    amax = np.abs(blocks).max(-1, keepdims=True)
    byte = np.maximum(np.where(amax > 0, np.frexp(amax)[1] - 1 + 127, 0) - down, 1)
    scale = np.exp2(byte - 127.0)
    codes = (blocks / scale).astype(np.float32).astype(dtype).astype(np.float64)
    return np.moveaxis((codes * scale).reshape(v.shape), -1, axis)


WIDE = False


def mx_kscale(k):
    if not WIDE:
        return np.ones(k)
    levels = np.array([24, -24, 12, -12, 0])
    if k % 512:
        return np.exp2(np.random.permutation(np.resize(levels, k // 32))).repeat(32)
    a = np.empty((k // 512, 16))
    for p in range(k // 512):
        a[p, :8] = np.random.permutation(np.resize(levels, 8))
        for g in range(8):
            far = levels[np.abs(levels - a[p, g]) >= 10]
            a[p, g + 8] = far[np.random.randint(len(far))]
    return np.exp2(a.ravel()).repeat(32)


def f64(x):
    return np.asarray(x).astype(np.float64)


def striped8(idx):
    return np.concatenate([v.reshape(-1, 16).T for v in idx]).astype(np.uint16)


def unstriped8(offs):
    return np.stack([offs[16 * g:16 * g + 16].T.reshape(-1) for g in range(8)]).astype(np.int64)


E2M1 = np.array([0.0, 0.5, 1.0, 1.5, 2.0, 3.0, 4.0, 6.0, -0.0, -0.5, -1.0, -1.5, -2.0, -3.0, -4.0, -6.0])


def pack_weight(w, fmt):
    k, n = w.shape
    w = f64(np.asarray(w, np.float32).astype(ml_dtypes.bfloat16)).reshape(k // 32, 32, n)
    amax = np.abs(w).max(1)
    if fmt == "e4m3":
        byte = np.frexp(amax)[1] - 1 + 127 - 7
    else:
        mant, ex = np.frexp(amax / 6.0)
        byte = np.where(mant > 0.5, ex, ex - 1) + 127
    byte = np.clip(np.where(amax > 0, byte, 1), 1, 254)
    scaled = (w * np.exp2(127.0 - byte)[:, None, :]).reshape(k, n).astype(np.float32)
    by_word = np.ascontiguousarray(scaled.reshape(k // 512, 128, 4, n).transpose(0, 1, 3, 2))
    if fmt == "e4m3":
        words = by_word.astype(ml_dtypes.float8_e4m3fn).view(np.uint8)
    else:
        c = by_word.astype(ml_dtypes.float4_e2m1fn).view(np.uint8) & 0xF
        words = (c[..., 0::2] | (c[..., 1::2] << 4)).reshape(k // 512, 128, 2 * n)
    return np.ascontiguousarray(words), np.ascontiguousarray(byte.astype(np.uint8).reshape(k // 512, 16, n))


def unpack_weight(words, scales, fmt):
    g, _, n = scales.shape
    words = np.ascontiguousarray(words).reshape(g, 128, n, -1)
    if fmt == "e4m3":
        vals = words.view(ml_dtypes.float8_e4m3fn).astype(np.float64)
    else:
        nib = np.empty((g, 128, n, 4), np.uint8)
        nib[..., 0::2] = words & 0xF
        nib[..., 1::2] = words >> 4
        vals = E2M1[nib]
    vals = vals * np.repeat(np.exp2(scales.astype(np.float64) - 127.0), 8, axis=1)[..., None]
    return vals.transpose(0, 1, 3, 2).reshape(g * 512, n)


def planes(y):
    n, m = y.shape
    v = y.astype(np.float32).astype(ml_dtypes.bfloat16).astype(np.float64).reshape(n // 32, 32, m)
    top = np.abs(v).max(1)
    byte = np.clip(np.where(top > 0, np.frexp(top)[1] - 1 + 127 - 7, 1), 1, 254)
    codes = (v * np.exp2(127.0 - byte)[:, None, :]).reshape(n, m).astype(np.float32).astype(ml_dtypes.float8_e4m3fn).view(np.uint8)
    words = codes.reshape(n // 512, 128, 4, m).transpose(0, 1, 3, 2)
    return np.ascontiguousarray(words), np.ascontiguousarray(byte.astype(np.uint8).reshape(n // 512, 16, m))


K, R, N, T, J = 1024, 1024, 512, 2048, 1024


def setup_inputs():
    n = np.random.standard_normal
    s = mx_kscale(K)[:, None]
    u = mx_kscale(R)[:, None]
    wd = n((R, N)) / np.sqrt(R) / u
    p_wg = pack_weight(n((K, R)) / np.sqrt(K) / s, "e4m3")
    p_wu = pack_weight(n((K, R)) / np.sqrt(K) / s * u.T, "e2m1")
    p_wd8 = pack_weight(wd[:512], "e4m3")
    p_wd4 = pack_weight(wd[512:], "e2m1")
    return {
        "xT": (n((K, T)) * s).astype(np.float32),
        "wgt": np.repeat(np.random.uniform(0.5, 2.0, (8, J)), 16, axis=0).astype(np.float32),
        "wg_words": p_wg[0],
        "wg_scales": p_wg[1],
        "wu_words": p_wu[0],
        "wu_scales": p_wu[1],
        "wd8_words": p_wd8[0],
        "wd8_scales": p_wd8[1],
        "wd4_words": p_wd4[0],
        "wd4_scales": p_wd4[1],
        "res": (n((N, J))).astype(np.float32),
        "offs": striped8(np.stack([np.random.permutation(T)[:J] for _ in range(8)])),
    }


def reference(xT, wgt, wg_words, wg_scales, wu_words, wu_scales, wd8_words, wd8_scales, wd4_words, wd4_scales, res, offs):
    idx = unstriped8(offs)
    rows = np.arange(K)
    xg = f64(wgt)[rows // 4 % 128] * f64(xT)[rows[:, None], idx[rows % 512 // 64]]
    xT_ = mxq(xg, 0, "e4m3")
    wg_ = unpack_weight(wg_words, wg_scales, "e4m3")
    wu_ = unpack_weight(wu_words, wu_scales, "e2m1")
    ga = wg_.T @ xT_
    ub = wu_.T @ xT_
    h = np.tanh(ga) * ub
    h_ = mxq(h, 0, "e4m3")
    wd8_ = unpack_weight(wd8_words, wd8_scales, "e4m3")
    wd4_ = unpack_weight(wd4_words, wd4_scales, "e2m1")
    y = wd8_.T @ h_[:512] + wd4_.T @ h_[512:]
    out_0 = f64(res) + y
    return (out_0,) + planes(out_0)

@@ -1,0 +1,291 @@
+from contextlib import ExitStack
+
+import concourse.mybir as mybir
+from concourse.masks import make_identity
+
+K, R, N, T, J = 1024, 1024, 512, 2048, 1024
+FLOPS = 2 * J * (2 * K * R + R * N)
+
+F32 = mybir.dt.float32
+BF16 = mybir.dt.bfloat16
+I32 = mybir.dt.int32
+U16 = mybir.dt.uint16
+U8 = mybir.dt.uint8
+E4M3 = mybir.dt.float8_e4m3fn_x4
+E2M1 = mybir.dt.float4_e2m1fn_x4
+MULT = mybir.AluOpType.mult
+ADD = mybir.AluOpType.add
+TANH = mybir.ActivationFunctionType.Tanh
+
+P = 128
+PACK = 4
+PASS = P * PACK
+TILE = 128
+TILES = J // TILE
+LATE_CHUNKS = (128, 128, 256, 256, 256)
+PAIR = 2 * TILE
+HALF = J // 2
+
+
+def round_and_weave(nc, woven, planes):
+    nc.scalar.copy(
+        out=woven.rearrange("p (c i) t -> p c t i", i=4),
+        in_=planes.rearrange("p t (c i) -> p c t i", i=4),
+    )
+
+
+def tile_list_tanh_mix_resP_kernel(
+    tc, xT, wgt, wg_words, wg_scales, wu_words, wu_scales, wd8_words, wd8_scales,
+    wd4_words, wd4_scales, res, offs, out_0, out_1, out_2,
+):
+    nc = tc.nc
+    x_rows = xT.rearrange("(a p i) t -> a i p t", a=2, i=PACK)
+    res_rows = res.rearrange("(p i) j -> p i j", i=PACK)
+    out_rows = out_0.rearrange("(p i) j -> p i j", i=PACK)
+    out_words = out_1[0].rearrange("p j i -> p (j i)").bitcast(I32)
+
+    with ExitStack() as ctx:
+        keep = ctx.enter_context(tc.tile_pool(name="keep", bufs=1))
+        ring = ctx.enter_context(tc.tile_pool(name="ring", bufs=2))
+        psum = ctx.enter_context(tc.psum_pool(name="psum", bufs=1))
+
+        offsets = keep.tile([P, J // 16], U16, name="offsets")
+        nc.sync.dma_start(offsets[:], offs)
+
+        up_planes = keep.tile([P, 2 * R], U8, name="up_planes", align_bytes=64)
+        down_planes_raw = keep.tile([P, N], U8, name="down_planes_raw", align_bytes=64)
+        nc.vector.memset(up_planes[:].bitcast(I32), 0)
+        nc.vector.memset(down_planes_raw[:].bitcast(I32), 0)
+        ident = keep.tile([P, P], F32, name="ident")
+        make_identity(nc, ident[:])
+        warm = keep.tile([P, 2], F32, name="warm")
+        nc.vector.memset(warm[:, 0:1], 0.0)
+        nc.scalar.activation(out=warm[:, 1:2], in_=warm[:, 0:1], func=TANH)
+
+        wd8_raw = keep.tile([P, N], I32, name="wd8_raw")
+        wd4_raw = keep.tile([P, 2 * N], U8, name="wd4_raw")
+        nc.sync.dma_start(wd8_raw[:], wd8_words[0].rearrange("p n i -> p (n i)").bitcast(I32))
+        nc.sync.dma_start(wd4_raw[:].bitcast(I32), wd4_words[0].bitcast(I32))
+
+        x_planes = [[keep.tile([P, T], F32, name="x_%d_%d" % (a, i)) for i in range(PACK)] for a in range(2)]
+        weights = [keep.tile([P, HALF], F32, name="weights_%d" % s) for s in range(2)]
+        wg = [keep.tile([P, R], I32, name="wg_%d" % a, align_bytes=64) for a in range(2)]
+        wu = [keep.tile([P, 2 * R], U8, name="wu_%d" % a, align_bytes=64) for a in range(2)]
+
+        def load_up_planes(q):
+            nc.sync.dma_start(
+                up_planes[32 * q : 32 * q + 4, :].bitcast(I32).rearrange("r (a n) -> r a n", a=2),
+                wu_scales[:, 4 * q : 4 * q + 4, :].bitcast(I32).rearrange("a r n -> r a n"),
+            )
+            nc.sync.dma_start(
+                up_planes[32 * q + 4 : 32 * q + 12, 0:R].bitcast(I32),
+                wg_scales[:, 4 * q : 4 * q + 4, :].bitcast(I32),
+            )
+
+        def load_up_words(a):
+            nc.sync.dma_start(wg[a][:], wg_words[a].rearrange("p r i -> p (r i)").bitcast(I32))
+            nc.sync.dma_start(wu[a][:].bitcast(I32), wu_words[a].bitcast(I32))
+
+        nc.sync.dma_start(x_planes[0][0][:], x_rows[0, 0])
+        for s in range(2):
+            nc.sync.dma_start(weights[s][:], wgt[:, s * HALF : (s + 1) * HALF])
+        for i in range(1, PACK):
+            nc.sync.dma_start(x_planes[0][i][:], x_rows[0, i])
+        for i in range(PACK - 1):
+            load_up_planes(i)
+            nc.sync.dma_start(x_planes[1][i][:], x_rows[1, i])
+        load_up_planes(PACK - 1)
+        load_up_words(0)
+        nc.sync.dma_start(x_planes[1][PACK - 1][:], x_rows[1, PACK - 1])
+        load_up_words(1)
+        for q in range(4):
+            nc.sync.dma_start(
+                down_planes_raw[32 * q : 32 * q + 4, :].bitcast(I32),
+                wd4_scales[0, 4 * q : 4 * q + 4, :].bitcast(I32),
+            )
+            nc.sync.dma_start(
+                down_planes_raw[32 * q + 4 : 32 * q + 8, :].bitcast(I32),
+                wd8_scales[0, 4 * q : 4 * q + 4, :].bitcast(I32),
+            )
+        res_pairs = [keep.tile([P, PACK, PAIR], F32, name="res_%d" % s) for s in range(J // PAIR)]
+        for s in range(J // PAIR):
+            nc.sync.dma_start(res_pairs[s][:], res_rows[:, :, s * PAIR : (s + 1) * PAIR])
+
+        wd8 = keep.tile([P, N], I32, name="wd8", align_bytes=64)
+        wd4 = keep.tile([P, 2 * N], U8, name="wd4", align_bytes=64)
+        down_planes = keep.tile([P, N], U8, name="down_planes", align_bytes=64)
+        nc.vector.tensor_copy(
+            out=wd8[:].rearrange("p (i m) -> p i m", i=PACK),
+            in_=wd8_raw[:].rearrange("p (m i) -> p i m", i=PACK),
+        )
+        nc.vector.tensor_copy(
+            out=wd4[:].rearrange("p (i m e) -> p i m e", i=PACK, e=2),
+            in_=wd4_raw[:].rearrange("p (m i e) -> p i m e", i=PACK, e=2),
+        )
+
+        xg_codes = [keep.tile([P, J], I32, name="xg_codes_%d" % a, align_bytes=64) for a in range(2)]
+        xg_scales = [keep.tile([P, J], U8, name="xg_scales_%d" % a, align_bytes=64) for a in range(2)]
+
+        def pick(picked, a, i, j0, width):
+            nc.vector.tensor_tensor(
+                picked[:, i, :],
+                x_planes[a][i][:].indirect(offsets[:, j0 // 16 : (j0 + width) // 16]),
+                weights[j0 // HALF][:, j0 % HALF : j0 % HALF + width],
+                MULT,
+            )
+
+        def quantise_picks(planes, a, j0, width, tag):
+            woven = ring.tile([P, width, PACK], BF16, name=tag, tag=tag, align_bytes=64)
+            round_and_weave(nc, woven[:], planes)
+            nc.vector.quantize_mx(
+                out=xg_codes[a][:, j0 : j0 + width].bitcast(E4M3),
+                scales=xg_scales[a][:, j0 : j0 + width],
+                in_=woven[:].rearrange("p j t -> p (j t)"),
+            )
+
+        early = [keep.tile([P, PACK, HALF], F32, name="early_%d" % s) for s in range(2)]
+        for i in range(PACK):
+            for s in range(2):
+                pick(early[s], 0, i, s * HALF, HALF)
+        for s in range(2):
+            quantise_picks(early[s][:], 0, s * HALF, HALF, "woven_early")
+
+        def late_chunk(c):
+            j0, width = sum(LATE_CHUNKS[:c]), LATE_CHUNKS[c]
+            late = ring.tile([P, PACK, width], F32, name="late", tag="late", bufs=4)
+            for i in range(PACK):
+                pick(late, 1, i, j0, width)
+            quantise_picks(late[:], 1, j0, width, "woven_late")
+
+        hidden = {}
+
+        def up_stage(jt):
+            cols = slice(jt * TILE, (jt + 1) * TILE)
+            for b in range(2):
+                ga = psum.tile([P, PASS], F32, name="ga", tag="ga", bufs=3)
+                ub = psum.tile([P, PASS], F32, name="ub", tag="ub", bufs=3)
+                for a in range(2):
+                    nc.tensor.matmul_mx(
+                        out=ga[:],
+                        lhsT=xg_codes[a][:, cols].bitcast(E4M3),
+                        lhsT_scale=xg_scales[a][:, cols],
+                        rhs=wg[a][:, b * PASS : (b + 1) * PASS].bitcast(E4M3),
+                        rhs_scale=up_planes[4 + 4 * a : P, b * PASS : (b + 1) * PASS],
+                        start=(a == 0),
+                        stop=(a == 1),
+                    )
+                for a in range(2):
+                    nc.tensor.matmul_mx(
+                        out=ub[:],
+                        lhsT=xg_codes[a][:, cols].bitcast(E4M3),
+                        lhsT_scale=xg_scales[a][:, cols],
+                        rhs=wu[a][:, 2 * b * PASS : 2 * (b + 1) * PASS].bitcast(E2M1),
+                        rhs_scale=up_planes[:, a * R + b * PASS : a * R + (b + 1) * PASS],
+                        start=(a == 0),
+                        stop=(a == 1),
+                    )
+                gate = ring.tile([P, PASS], F32, name="gate", tag="gate", bufs=3)
+                nc.scalar.activation(
+                    out=gate[:].rearrange("j (u p e) -> j u p e", u=2, e=2),
+                    in_=ga[:].rearrange("j (p u e) -> j u p e", u=2, e=2),
+                    func=TANH,
+                )
+                h_rows = ring.tile([P, PASS], BF16, name="h_rows", tag="h_rows", bufs=4)
+                nc.vector.tensor_tensor(
+                    h_rows[:].rearrange("j (u p e) -> j u p e", u=2, e=2),
+                    ub[:].rearrange("j (p u e) -> j u p e", u=2, e=2),
+                    gate[:].rearrange("j (u p e) -> j u p e", u=2, e=2),
+                    MULT,
+                )
+                hidden[jt, b] = h_rows
+
+        h_quantised = {}
+
+        def turn_stage(jt):
+            turned = psum.tile([P, 2, 2, TILE], F32, name="turned", tag="turned")
+            for b in range(2):
+                pairs = hidden[jt, b][:].bitcast(F32)
+                for u in range(2):
+                    nc.tensor.transpose(turned[:, b, u, :], pairs[:, u * P : (u + 1) * P], ident[:])
+            h_woven = ring.tile([P, 2 * TILE * PACK], BF16, name="h_woven", tag="h_woven", align_bytes=64)
+            nc.scalar.copy(
+                out=h_woven[:].bitcast(F32).rearrange("p (b j u) -> p b j u", b=2, u=2),
+                in_=turned[:].rearrange("p b u j -> p b j u"),
+            )
+            h_codes = ring.tile([P, 2 * TILE], I32, name="h_codes", tag="h_codes", align_bytes=64)
+            h_scales = ring.tile([P, 2 * TILE], U8, name="h_scales", tag="h_scales", align_bytes=64)
+            nc.vector.quantize_mx(out=h_codes[:].bitcast(E4M3), scales=h_scales[:], in_=h_woven[:])
+            h_quantised[jt] = (h_codes, h_scales)
+
+        out_codes = keep.tile([P, J], I32, name="out_codes", align_bytes=64)
+        out_scales = keep.tile([P, J], U8, name="out_scales", align_bytes=64)
+        out_pairs = [keep.tile([P, PACK, PAIR], F32, name="out_%d" % s) for s in range(J // PAIR)]
+
+        def hand_on(planes, j0, width):
+            out_woven = ring.tile([P, width, PACK], BF16, name="out_woven", tag="out_woven", align_bytes=64)
+            round_and_weave(nc, out_woven[:], planes)
+            nc.vector.quantize_mx(
+                out=out_codes[:, j0 : j0 + width].bitcast(E4M3),
+                scales=out_scales[:, j0 : j0 + width],
+                in_=out_woven[:].rearrange("p j t -> p (j t)"),
+            )
+
+        def down_stage(jt):
+            h_codes, h_scales = h_quantised[jt]
+            y = psum.tile([P, PACK, TILE], F32, name="y", tag="y")
+            for i in range(PACK):
+                nc.tensor.matmul_mx(
+                    out=y[:, i, :],
+                    lhsT=wd8[:, i * P : (i + 1) * P].bitcast(E4M3),
+                    lhsT_scale=down_planes[4:P, i * P : (i + 1) * P],
+                    rhs=h_codes[:, 0:TILE].bitcast(E4M3),
+                    rhs_scale=h_scales[:, 0:TILE],
+                    start=True,
+                    stop=False,
+                )
+                nc.tensor.matmul_mx(
+                    out=y[:, i, :],
+                    lhsT=wd4[:, 2 * i * P : 2 * (i + 1) * P].bitcast(E2M1),
+                    lhsT_scale=down_planes[:, i * P : (i + 1) * P],
+                    rhs=h_codes[:, TILE : 2 * TILE].bitcast(E4M3),
+                    rhs_scale=h_scales[:, TILE : 2 * TILE],
+                    start=False,
+                    stop=True,
+                )
+            s, side = divmod(jt, 2)
+            part = slice(side * TILE, (side + 1) * TILE)
+            cols = slice(jt * TILE, (jt + 1) * TILE)
+            nc.vector.tensor_tensor(out_pairs[s][:, :, part], y[:], res_pairs[s][:, :, part], ADD)
+            last_pair = s == J // PAIR - 1
+            if last_pair:
+                nc.sync.dma_start(out_rows[:, :, cols], out_pairs[s][:, :, part])
+            elif side == 1:
+                nc.sync.dma_start(out_rows[:, :, s * PAIR : (s + 1) * PAIR], out_pairs[s][:])
+            if last_pair:
+                hand_on(out_pairs[s][:, :, part], jt * TILE, TILE)
+            elif side == 1:
+                hand_on(out_pairs[s][:], s * PAIR, PAIR)
+            if side == 1:
+                nc.sync.dma_start(out_words[:, s * PAIR : (s + 1) * PAIR], out_codes[:, s * PAIR : (s + 1) * PAIR])
+
+        late_chunk(0)
+        late_chunk(1)
+        late_chunk(2)
+        nc.vector.tensor_copy(
+            out=down_planes[:].rearrange("p (i m) -> p i m", i=PACK),
+            in_=down_planes_raw[:].rearrange("p (m i) -> p i m", i=PACK),
+        )
+        for step in range(TILES + 2):
+            if step < TILES:
+                up_stage(step)
+            if 1 <= step <= TILES:
+                turn_stage(step - 1)
+            if step >= 2:
+                down_stage(step - 2)
+            if step in (1, 3):
+                late_chunk(3 + step // 2)
+        for q in range(4):
+            nc.sync.dma_start(
+                out_2[0, 4 * q : 4 * q + 4, :].bitcast(I32),
+                out_scales[32 * q : 32 * q + 4, :].bitcast(I32),
+            )

@@ -22,9 +22,11 @@ PACK = 4
 PASS = P * PACK
 TILE = 128
 TILES = J // TILE
-LATE_CHUNKS = (128, 128, 256, 256, 256)
+LATE_CHUNKS = (128, 128, 128, 128, 256, 256)
 PAIR = 2 * TILE
 HALF = J // 2
+BANKS = {"ga": 3, "ub": 3, "turned": 1, "y": 1}
+HOLD = 4
 
 
 def round_and_weave(nc, woven, planes):
@@ -64,8 +66,6 @@ def tile_list_tanh_mix_resP_kernel(
 
         wd8_raw = keep.tile([P, N], I32, name="wd8_raw")
         wd4_raw = keep.tile([P, 2 * N], U8, name="wd4_raw")
-        nc.sync.dma_start(wd8_raw[:], wd8_words[0].rearrange("p n i -> p (n i)").bitcast(I32))
-        nc.sync.dma_start(wd4_raw[:].bitcast(I32), wd4_words[0].bitcast(I32))
 
         x_planes = [[keep.tile([P, T], F32, name="x_%d_%d" % (a, i)) for i in range(PACK)] for a in range(2)]
         weights = [keep.tile([P, HALF], F32, name="weights_%d" % s) for s in range(2)]
@@ -98,31 +98,28 @@ def tile_list_tanh_mix_resP_kernel(
         load_up_words(0)
         nc.sync.dma_start(x_planes[1][PACK - 1][:], x_rows[1, PACK - 1])
         load_up_words(1)
-        for q in range(4):
-            nc.sync.dma_start(
-                down_planes_raw[32 * q : 32 * q + 4, :].bitcast(I32),
-                wd4_scales[0, 4 * q : 4 * q + 4, :].bitcast(I32),
-            )
-            nc.sync.dma_start(
-                down_planes_raw[32 * q + 4 : 32 * q + 8, :].bitcast(I32),
-                wd8_scales[0, 4 * q : 4 * q + 4, :].bitcast(I32),
-            )
+        def load_down():
+            nc.sync.dma_start(wd8_raw[:], wd8_words[0].rearrange("p n i -> p (n i)").bitcast(I32))
+            nc.sync.dma_start(wd4_raw[:].bitcast(I32), wd4_words[0].bitcast(I32))
+            for q in range(4):
+                nc.sync.dma_start(
+                    down_planes_raw[32 * q : 32 * q + 4, :].bitcast(I32),
+                    wd4_scales[0, 4 * q : 4 * q + 4, :].bitcast(I32),
+                )
+                nc.sync.dma_start(
+                    down_planes_raw[32 * q + 4 : 32 * q + 8, :].bitcast(I32),
+                    wd8_scales[0, 4 * q : 4 * q + 4, :].bitcast(I32),
+                )
+
         res_pairs = [keep.tile([P, PACK, PAIR], F32, name="res_%d" % s) for s in range(J // PAIR)]
         for s in range(J // PAIR):
             nc.sync.dma_start(res_pairs[s][:], res_rows[:, :, s * PAIR : (s + 1) * PAIR])
+            if s == 1:
+                load_down()
 
         wd8 = keep.tile([P, N], I32, name="wd8", align_bytes=64)
         wd4 = keep.tile([P, 2 * N], U8, name="wd4", align_bytes=64)
         down_planes = keep.tile([P, N], U8, name="down_planes", align_bytes=64)
-        nc.vector.tensor_copy(
-            out=wd8[:].rearrange("p (i m) -> p i m", i=PACK),
-            in_=wd8_raw[:].rearrange("p (m i) -> p i m", i=PACK),
-        )
-        nc.vector.tensor_copy(
-            out=wd4[:].rearrange("p (i m e) -> p i m e", i=PACK, e=2),
-            in_=wd4_raw[:].rearrange("p (m i e) -> p i m e", i=PACK, e=2),
-        )
-
         xg_codes = [keep.tile([P, J], I32, name="xg_codes_%d" % a, align_bytes=64) for a in range(2)]
         xg_scales = [keep.tile([P, J], U8, name="xg_scales_%d" % a, align_bytes=64) for a in range(2)]
 
@@ -150,20 +147,42 @@ def tile_list_tanh_mix_resP_kernel(
         for s in range(2):
             quantise_picks(early[s][:], 0, s * HALF, HALF, "woven_early")
 
+        late = [
+            keep.tile([P, PACK + 1, width], F32, name="late_%d" % c, align_bytes=64)
+            for c, width in enumerate(LATE_CHUNKS)
+        ]
+        for i in range(PACK - 1):
+            for c, width in enumerate(LATE_CHUNKS):
+                pick(late[c], 1, i, sum(LATE_CHUNKS[:c]), width)
+
+        def late_pick(c):
+            pick(late[c], 1, PACK - 1, sum(LATE_CHUNKS[:c]), LATE_CHUNKS[c])
+
         def late_chunk(c):
             j0, width = sum(LATE_CHUNKS[:c]), LATE_CHUNKS[c]
-            late = ring.tile([P, PACK, width], F32, name="late", tag="late", bufs=4)
-            for i in range(PACK):
-                pick(late, 1, i, j0, width)
-            quantise_picks(late[:], 1, j0, width, "woven_late")
+            if c + HOLD < len(LATE_CHUNKS):
+                room = late[c + HOLD][:, PACK - 1 :, :].rearrange("p t j -> p (t j)").bitcast(BF16)
+                woven = room[:, 0 : PACK * width].rearrange("p (j t) -> p j t", t=PACK)
+            else:
+                spare = ring.tile([P, width, PACK], BF16, name="woven_late", tag="woven_late", align_bytes=64)
+                woven = spare[:]
+            round_and_weave(nc, woven, late[c][:, 0:PACK, :])
+            nc.vector.quantize_mx(
+                out=xg_codes[1][:, j0 : j0 + width].bitcast(E4M3),
+                scales=xg_scales[1][:, j0 : j0 + width],
+                in_=woven.rearrange("p j t -> p (j t)"),
+            )
+            if c + HOLD < len(LATE_CHUNKS):
+                late_pick(c + HOLD)
 
         hidden = {}
 
         def up_stage(jt):
             cols = slice(jt * TILE, (jt + 1) * TILE)
             for b in range(2):
-                ga = psum.tile([P, PASS], F32, name="ga", tag="ga", bufs=3)
-                ub = psum.tile([P, PASS], F32, name="ub", tag="ub", bufs=3)
+                ga_tag, ub_tag = ("turned", "y") if (jt, b) == (1, 1) else ("ga", "ub")
+                ga = psum.tile([P, PASS], F32, name="ga", tag=ga_tag, bufs=BANKS[ga_tag])
+                ub = psum.tile([P, PASS], F32, name="ub", tag=ub_tag, bufs=BANKS[ub_tag])
                 for a in range(2):
                     nc.tensor.matmul_mx(
                         out=ga[:],
@@ -190,7 +209,7 @@ def tile_list_tanh_mix_resP_kernel(
                     in_=ga[:].rearrange("j (p u e) -> j u p e", u=2, e=2),
                     func=TANH,
                 )
-                h_rows = ring.tile([P, PASS], BF16, name="h_rows", tag="h_rows", bufs=4)
+                h_rows = ring.tile([P, PASS], BF16, name="h_rows", tag="h_rows", bufs=6)
                 nc.vector.tensor_tensor(
                     h_rows[:].rearrange("j (u p e) -> j u p e", u=2, e=2),
                     ub[:].rearrange("j (p u e) -> j u p e", u=2, e=2),
@@ -201,25 +220,41 @@ def tile_list_tanh_mix_resP_kernel(
 
         h_quantised = {}
 
-        def turn_stage(jt):
-            turned = psum.tile([P, 2, 2, TILE], F32, name="turned", tag="turned")
-            for b in range(2):
+        def turn_stage(jt, halves=(0, 1), tag="turned"):
+            count = len(halves)
+            turned = psum.tile([P, count, 2, TILE], F32, name="turned", tag=tag, bufs=BANKS[tag])
+            for n, b in enumerate(halves):
                 pairs = hidden[jt, b][:].bitcast(F32)
                 for u in range(2):
-                    nc.tensor.transpose(turned[:, b, u, :], pairs[:, u * P : (u + 1) * P], ident[:])
-            h_woven = ring.tile([P, 2 * TILE * PACK], BF16, name="h_woven", tag="h_woven", align_bytes=64)
+                    nc.tensor.transpose(turned[:, n, u, :], pairs[:, u * P : (u + 1) * P], ident[:])
+            h_woven = ring.tile([P, count * TILE * PACK], BF16, name="h_woven", tag="h_woven", bufs=3, align_bytes=64)
             nc.scalar.copy(
-                out=h_woven[:].bitcast(F32).rearrange("p (b j u) -> p b j u", b=2, u=2),
+                out=h_woven[:].bitcast(F32).rearrange("p (b j u) -> p b j u", b=count, u=2),
                 in_=turned[:].rearrange("p b u j -> p b j u"),
             )
-            h_codes = ring.tile([P, 2 * TILE], I32, name="h_codes", tag="h_codes", align_bytes=64)
-            h_scales = ring.tile([P, 2 * TILE], U8, name="h_scales", tag="h_scales", align_bytes=64)
+            h_codes = ring.tile([P, count * TILE], I32, name="h_codes", tag="h_codes", bufs=4, align_bytes=64)
+            h_scales = ring.tile([P, count * TILE], U8, name="h_scales", tag="h_scales", bufs=4, align_bytes=64)
             nc.vector.quantize_mx(out=h_codes[:].bitcast(E4M3), scales=h_scales[:], in_=h_woven[:])
-            h_quantised[jt] = (h_codes, h_scales)
+            for n, b in enumerate(halves):
+                h_quantised[jt, b] = (h_codes[:, n * TILE : (n + 1) * TILE], h_scales[:, n * TILE : (n + 1) * TILE])
 
         out_codes = keep.tile([P, J], I32, name="out_codes", align_bytes=64)
         out_scales = keep.tile([P, J], U8, name="out_scales", align_bytes=64)
         out_pairs = [keep.tile([P, PACK, PAIR], F32, name="out_%d" % s) for s in range(J // PAIR)]
+
+        def deal_down_weights():
+            nc.vector.tensor_copy(
+                out=wd8[:].rearrange("p (i m) -> p i m", i=PACK),
+                in_=wd8_raw[:].rearrange("p (m i) -> p i m", i=PACK),
+            )
+            nc.vector.tensor_copy(
+                out=wd4[:].bitcast(U16).rearrange("p (i m) -> p i m", i=PACK),
+                in_=wd4_raw[:].bitcast(U16).rearrange("p (m i) -> p i m", i=PACK),
+            )
+            nc.vector.tensor_copy(
+                out=down_planes[:].rearrange("p (i m) -> p i m", i=PACK),
+                in_=down_planes_raw[:].rearrange("p (m i) -> p i m", i=PACK),
+            )
 
         def hand_on(planes, j0, width):
             out_woven = ring.tile([P, width, PACK], BF16, name="out_woven", tag="out_woven", align_bytes=64)
@@ -230,62 +265,101 @@ def tile_list_tanh_mix_resP_kernel(
                 in_=out_woven[:].rearrange("p j t -> p (j t)"),
             )
 
-        def down_stage(jt):
-            h_codes, h_scales = h_quantised[jt]
-            y = psum.tile([P, PACK, TILE], F32, name="y", tag="y")
+        sums = {}
+
+        def down_pass(jt, b, i, start, stop):
+            codes, scales = h_quantised[jt, b]
+            if b == 0:
+                lhsT = wd8[:, i * P : (i + 1) * P].bitcast(E4M3)
+                lhsT_scale = down_planes[4:P, i * P : (i + 1) * P]
+            else:
+                lhsT = wd4[:, 2 * i * P : 2 * (i + 1) * P].bitcast(E2M1)
+                lhsT_scale = down_planes[:, i * P : (i + 1) * P]
+            nc.tensor.matmul_mx(
+                out=sums[jt][:, i, :], lhsT=lhsT, lhsT_scale=lhsT_scale,
+                rhs=codes.bitcast(E4M3), rhs_scale=scales, start=start, stop=stop,
+            )
+
+        def down_half(jt, b, tag="y"):
+            if b == 0:
+                sums[jt] = psum.tile([P, PACK, TILE], F32, name="y", tag=tag, bufs=BANKS[tag])
             for i in range(PACK):
-                nc.tensor.matmul_mx(
-                    out=y[:, i, :],
-                    lhsT=wd8[:, i * P : (i + 1) * P].bitcast(E4M3),
-                    lhsT_scale=down_planes[4:P, i * P : (i + 1) * P],
-                    rhs=h_codes[:, 0:TILE].bitcast(E4M3),
-                    rhs_scale=h_scales[:, 0:TILE],
-                    start=True,
-                    stop=False,
-                )
-                nc.tensor.matmul_mx(
-                    out=y[:, i, :],
-                    lhsT=wd4[:, 2 * i * P : 2 * (i + 1) * P].bitcast(E2M1),
-                    lhsT_scale=down_planes[:, i * P : (i + 1) * P],
-                    rhs=h_codes[:, TILE : 2 * TILE].bitcast(E4M3),
-                    rhs_scale=h_scales[:, TILE : 2 * TILE],
-                    start=False,
-                    stop=True,
-                )
+                down_pass(jt, b, i, b == 0 and i == 0, b == 1 and i == PACK - 1)
+
+        def add_residual(jt, j0, width):
+            s, side = divmod(jt, 2)
+            part = slice(side * TILE + j0, side * TILE + j0 + width)
+            nc.vector.tensor_tensor(
+                out_pairs[s][:, :, part], sums[jt][:, :, j0 : j0 + width], res_pairs[s][:, :, part], ADD
+            )
+
+        def store_rows(jt):
             s, side = divmod(jt, 2)
             part = slice(side * TILE, (side + 1) * TILE)
-            cols = slice(jt * TILE, (jt + 1) * TILE)
-            nc.vector.tensor_tensor(out_pairs[s][:, :, part], y[:], res_pairs[s][:, :, part], ADD)
-            last_pair = s == J // PAIR - 1
-            if last_pair:
-                nc.sync.dma_start(out_rows[:, :, cols], out_pairs[s][:, :, part])
+            if s == J // PAIR - 1:
+                nc.sync.dma_start(out_rows[:, :, jt * TILE : (jt + 1) * TILE], out_pairs[s][:, :, part])
             elif side == 1:
                 nc.sync.dma_start(out_rows[:, :, s * PAIR : (s + 1) * PAIR], out_pairs[s][:])
-            if last_pair:
+
+        def down_stage(jt, tag="y"):
+            down_half(jt, 0, tag)
+            down_half(jt, 1)
+            add_residual(jt, 0, TILE)
+            store_rows(jt)
+
+        def store_planes(j0, width):
+            nc.sync.dma_start(out_words[:, j0 : j0 + width], out_codes[:, j0 : j0 + width])
+
+        def store_scales(j0, width, queue):
+            for q in range(4):
+                queue.dma_start(
+                    out_2[0, 4 * q : 4 * q + 4, j0 : j0 + width].bitcast(I32),
+                    out_scales[32 * q : 32 * q + 4, j0 : j0 + width].bitcast(I32),
+                )
+
+        def hand_on_stage(jt):
+            s, side = divmod(jt, 2)
+            part = slice(side * TILE, (side + 1) * TILE)
+            if s >= 2:
                 hand_on(out_pairs[s][:, :, part], jt * TILE, TILE)
             elif side == 1:
                 hand_on(out_pairs[s][:], s * PAIR, PAIR)
             if side == 1:
-                nc.sync.dma_start(out_words[:, s * PAIR : (s + 1) * PAIR], out_codes[:, s * PAIR : (s + 1) * PAIR])
+                store_planes(s * PAIR, PAIR)
 
-        late_chunk(0)
-        late_chunk(1)
-        late_chunk(2)
-        nc.vector.tensor_copy(
-            out=down_planes[:].rearrange("p (i m) -> p i m", i=PACK),
-            in_=down_planes_raw[:].rearrange("p (m i) -> p i m", i=PACK),
-        )
-        for step in range(TILES + 2):
-            if step < TILES:
-                up_stage(step)
-            if 1 <= step <= TILES:
+        for c in range(HOLD):
+            late_pick(c)
+        for c in range(3):
+            late_chunk(c)
+        last = TILES - 1
+        for step in range(TILES):
+            up_stage(step)
+            if step + 3 < len(LATE_CHUNKS):
+                late_chunk(step + 3)
+            if step == 1:
+                deal_down_weights()
+            if step >= 1 and step < last:
                 turn_stage(step - 1)
-            if step >= 2:
+            if step >= 2 and step < last:
                 down_stage(step - 2)
-            if step in (1, 3):
-                late_chunk(3 + step // 2)
-        for q in range(4):
-            nc.sync.dma_start(
-                out_2[0, 4 * q : 4 * q + 4, :].bitcast(I32),
-                out_scales[32 * q : 32 * q + 4, :].bitcast(I32),
-            )
+            if step >= 3 and step < last:
+                hand_on_stage(step - 3)
+        turn_stage(6)
+        turn_stage(7, (0,), "ga")
+        turn_stage(7, (1,), "ub")
+        down_stage(5)
+        down_stage(6, "ga")
+        down_half(7, 0, "ub")
+        down_half(7, 1)
+        hand_on_stage(4)
+        hand_on_stage(5)
+        store_scales(0, J - PAIR, nc.sync)
+        hand_on_stage(6)
+        s, side = divmod(last, 2)
+        for j0 in (0, TILE // 2):
+            add_residual(last, j0, TILE // 2)
+        store_rows(last)
+        for j0 in (0, TILE // 2):
+            hand_on(out_pairs[s][:, :, side * TILE + j0 : side * TILE + j0 + TILE // 2], last * TILE + j0, TILE // 2)
+        store_planes(s * PAIR, PAIR)
+        store_scales(J - PAIR, PAIR, nc.scalar)

@@ -25,6 +25,8 @@ TILES = J // TILE
 LATE_CHUNKS = (128, 128, 128, 128, 256, 256)
 PAIR = 2 * TILE
 HALF = J // 2
+GATES_FIRST = 8
+LENT = {(2, 1): 0, (3, 0): 1, (3, 1): 2, (4, 0): 3}
 BANKS = {"ga": 3, "ub": 3, "turned": 1, "y": 1}
 HOLD = 4
 
@@ -68,7 +70,7 @@ def tile_list_tanh_mix_resP_kernel(
         wd4_raw = keep.tile([P, 2 * N], U8, name="wd4_raw")
 
         x_planes = [[keep.tile([P, T], F32, name="x_%d_%d" % (a, i)) for i in range(PACK)] for a in range(2)]
-        weights = [keep.tile([P, HALF], F32, name="weights_%d" % s) for s in range(2)]
+        weights = keep.tile([P, J], F32, name="weights")
         wg = [keep.tile([P, R], I32, name="wg_%d" % a, align_bytes=64) for a in range(2)]
         wu = [keep.tile([P, 2 * R], U8, name="wu_%d" % a, align_bytes=64) for a in range(2)]
 
@@ -86,18 +88,29 @@ def tile_list_tanh_mix_resP_kernel(
             nc.sync.dma_start(wg[a][:], wg_words[a].rearrange("p r i -> p (r i)").bitcast(I32))
             nc.sync.dma_start(wu[a][:].bitcast(I32), wu_words[a].bitcast(I32))
 
-        nc.sync.dma_start(x_planes[0][0][:], x_rows[0, 0])
+        def load_x(a, i):
+            nc.sync.dma_start(x_planes[a][i][:], x_rows[a, i])
+
+        def load_wg(a):
+            nc.sync.dma_start(wg[a][:], wg_words[a].rearrange("p r i -> p (r i)").bitcast(I32))
+
+        def load_wu(a):
+            nc.sync.dma_start(wu[a][:].bitcast(I32), wu_words[a].bitcast(I32))
+
+        load_x(0, 0)
         for s in range(2):
-            nc.sync.dma_start(weights[s][:], wgt[:, s * HALF : (s + 1) * HALF])
+            nc.sync.dma_start(weights[:, s * HALF : (s + 1) * HALF], wgt[:, s * HALF : (s + 1) * HALF])
         for i in range(1, PACK):
-            nc.sync.dma_start(x_planes[0][i][:], x_rows[0, i])
+            load_x(0, i)
         for i in range(PACK - 1):
             load_up_planes(i)
-            nc.sync.dma_start(x_planes[1][i][:], x_rows[1, i])
+            load_x(1, i)
         load_up_planes(PACK - 1)
-        load_up_words(0)
-        nc.sync.dma_start(x_planes[1][PACK - 1][:], x_rows[1, PACK - 1])
-        load_up_words(1)
+        load_wg(0)
+        load_x(1, 3)
+        load_wu(0)
+        load_wg(1)
+        load_wu(1)
         def load_down():
             nc.sync.dma_start(wd8_raw[:], wd8_words[0].rearrange("p n i -> p (n i)").bitcast(I32))
             nc.sync.dma_start(wd4_raw[:].bitcast(I32), wd4_words[0].bitcast(I32))
@@ -127,7 +140,7 @@ def tile_list_tanh_mix_resP_kernel(
             nc.vector.tensor_tensor(
                 picked[:, i, :],
                 x_planes[a][i][:].indirect(offsets[:, j0 // 16 : (j0 + width) // 16]),
-                weights[j0 // HALF][:, j0 % HALF : j0 % HALF + width],
+                weights[:, j0 : j0 + width],
                 MULT,
             )
 
@@ -140,27 +153,29 @@ def tile_list_tanh_mix_resP_kernel(
                 in_=woven[:].rearrange("p j t -> p (j t)"),
             )
 
-        early = [keep.tile([P, PACK, HALF], F32, name="early_%d" % s) for s in range(2)]
+        early = keep.tile([P, PACK, J], F32, name="early")
         for i in range(PACK):
-            for s in range(2):
-                pick(early[s], 0, i, s * HALF, HALF)
+            for j0 in ((0, HALF) if i in (0, PACK - 1) else (0,)):
+                width = HALF if i in (0, PACK - 1) else J
+                pick(early[:, :, j0 : j0 + width], 0, i, j0, width)
         for s in range(2):
-            quantise_picks(early[s][:], 0, s * HALF, HALF, "woven_early")
+            quantise_picks(early[:, :, s * HALF : (s + 1) * HALF], 0, s * HALF, HALF, "woven_early")
 
-        late = [
-            keep.tile([P, PACK + 1, width], F32, name="late_%d" % c, align_bytes=64)
-            for c, width in enumerate(LATE_CHUNKS)
-        ]
+        late_first = keep.tile([P, PACK, HALF], F32, name="late_first")
+        late_next = keep.tile([P, PACK + 1, PAIR], F32, name="late_next", align_bytes=64)
+        late_last = keep.tile([P, PACK, PASS], F32, name="late_last")
+        late = [late_first[:, :, c * TILE : (c + 1) * TILE] for c in range(HOLD)]
+        late.extend([late_next, late_last[:, :, 0:PAIR]])
         for i in range(PACK - 1):
-            for c, width in enumerate(LATE_CHUNKS):
-                pick(late[c], 1, i, sum(LATE_CHUNKS[:c]), width)
+            pick(late_first, 1, i, 0, HALF)
+            pick(late_next, 1, i, HALF, PAIR)
 
         def late_pick(c):
             pick(late[c], 1, PACK - 1, sum(LATE_CHUNKS[:c]), LATE_CHUNKS[c])
 
         def late_chunk(c):
             j0, width = sum(LATE_CHUNKS[:c]), LATE_CHUNKS[c]
-            if c + HOLD < len(LATE_CHUNKS):
+            if c + HOLD < len(LATE_CHUNKS) - 1:
                 room = late[c + HOLD][:, PACK - 1 :, :].rearrange("p t j -> p (t j)").bitcast(BF16)
                 woven = room[:, 0 : PACK * width].rearrange("p (j t) -> p j t", t=PACK)
             else:
@@ -172,51 +187,74 @@ def tile_list_tanh_mix_resP_kernel(
                 scales=xg_scales[1][:, j0 : j0 + width],
                 in_=woven.rearrange("p j t -> p (j t)"),
             )
-            if c + HOLD < len(LATE_CHUNKS):
+            if c + HOLD < len(LATE_CHUNKS) - 1:
                 late_pick(c + HOLD)
 
         hidden = {}
 
-        def up_stage(jt):
+        gates = {}
+
+        def gate_unit(jt, b):
             cols = slice(jt * TILE, (jt + 1) * TILE)
-            for b in range(2):
-                ga_tag, ub_tag = ("turned", "y") if (jt, b) == (1, 1) else ("ga", "ub")
-                ga = psum.tile([P, PASS], F32, name="ga", tag=ga_tag, bufs=BANKS[ga_tag])
-                ub = psum.tile([P, PASS], F32, name="ub", tag=ub_tag, bufs=BANKS[ub_tag])
-                for a in range(2):
-                    nc.tensor.matmul_mx(
-                        out=ga[:],
-                        lhsT=xg_codes[a][:, cols].bitcast(E4M3),
-                        lhsT_scale=xg_scales[a][:, cols],
-                        rhs=wg[a][:, b * PASS : (b + 1) * PASS].bitcast(E4M3),
-                        rhs_scale=up_planes[4 + 4 * a : P, b * PASS : (b + 1) * PASS],
-                        start=(a == 0),
-                        stop=(a == 1),
-                    )
-                for a in range(2):
-                    nc.tensor.matmul_mx(
-                        out=ub[:],
-                        lhsT=xg_codes[a][:, cols].bitcast(E4M3),
-                        lhsT_scale=xg_scales[a][:, cols],
-                        rhs=wu[a][:, 2 * b * PASS : 2 * (b + 1) * PASS].bitcast(E2M1),
-                        rhs_scale=up_planes[:, a * R + b * PASS : a * R + (b + 1) * PASS],
-                        start=(a == 0),
-                        stop=(a == 1),
-                    )
+            tag = "turned" if (jt, b) == (1, 1) else "ga"
+            ga = psum.tile([P, PASS], F32, name="ga", tag=tag, bufs=BANKS[tag])
+            for a in range(2):
+                nc.tensor.matmul_mx(
+                    out=ga[:],
+                    lhsT=xg_codes[a][:, cols].bitcast(E4M3),
+                    lhsT_scale=xg_scales[a][:, cols],
+                    rhs=wg[a][:, b * PASS : (b + 1) * PASS].bitcast(E4M3),
+                    rhs_scale=up_planes[4 + 4 * a : P, b * PASS : (b + 1) * PASS],
+                    start=(a == 0),
+                    stop=(a == 1),
+                )
+            if (jt, b) in LENT:
+                gate = late_last[:, LENT[jt, b], :]
+            else:
                 gate = ring.tile([P, PASS], F32, name="gate", tag="gate", bufs=3)
-                nc.scalar.activation(
-                    out=gate[:].rearrange("j (u p e) -> j u p e", u=2, e=2),
-                    in_=ga[:].rearrange("j (p u e) -> j u p e", u=2, e=2),
-                    func=TANH,
+            nc.scalar.activation(
+                out=gate[:].rearrange("j (u p e) -> j u p e", u=2, e=2),
+                in_=ga[:].rearrange("j (p u e) -> j u p e", u=2, e=2),
+                func=TANH,
+            )
+            gates[jt, b] = gate
+
+        def up_unit(jt, b):
+            cols = slice(jt * TILE, (jt + 1) * TILE)
+            tag = "y" if (jt, b) == (1, 1) else "ub"
+            ub = psum.tile([P, PASS], F32, name="ub", tag=tag, bufs=BANKS[tag])
+            for a in range(2):
+                nc.tensor.matmul_mx(
+                    out=ub[:],
+                    lhsT=xg_codes[a][:, cols].bitcast(E4M3),
+                    lhsT_scale=xg_scales[a][:, cols],
+                    rhs=wu[a][:, 2 * b * PASS : 2 * (b + 1) * PASS].bitcast(E2M1),
+                    rhs_scale=up_planes[:, a * R + b * PASS : a * R + (b + 1) * PASS],
+                    start=(a == 0),
+                    stop=(a == 1),
                 )
-                h_rows = ring.tile([P, PASS], BF16, name="h_rows", tag="h_rows", bufs=6)
-                nc.vector.tensor_tensor(
-                    h_rows[:].rearrange("j (u p e) -> j u p e", u=2, e=2),
-                    ub[:].rearrange("j (p u e) -> j u p e", u=2, e=2),
-                    gate[:].rearrange("j (u p e) -> j u p e", u=2, e=2),
-                    MULT,
-                )
-                hidden[jt, b] = h_rows
+            h_rows = ring.tile([P, PASS], BF16, name="h_rows", tag="h_rows", bufs=6)
+            nc.vector.tensor_tensor(
+                h_rows[:].rearrange("j (u p e) -> j u p e", u=2, e=2),
+                ub[:].rearrange("j (p u e) -> j u p e", u=2, e=2),
+                gates[jt, b][:].rearrange("j (u p e) -> j u p e", u=2, e=2),
+                MULT,
+            )
+            hidden[jt, b] = h_rows
+            if (jt, b) in LENT:
+                pick(late[-1], 1, LENT[jt, b], J - LATE_CHUNKS[-1], LATE_CHUNKS[-1])
+                if LENT[jt, b] == PACK - 1:
+                    late_chunk(len(LATE_CHUNKS) - 1)
+
+        def up_stage(jt):
+            if jt >= GATES_FIRST:
+                for unit in (gate_unit, up_unit):
+                    for b in range(2):
+                        unit(jt, b)
+            else:
+                for b in range(2):
+                    gate_unit(jt, b)
+                    up_unit(jt, b)
 
         h_quantised = {}
 
@@ -332,10 +370,13 @@ def tile_list_tanh_mix_resP_kernel(
         for c in range(3):
             late_chunk(c)
         last = TILES - 1
+        res_woven = keep.tile([P, TILE, PACK], F32, name="res_woven")
         for step in range(TILES):
             up_stage(step)
-            if step + 3 < len(LATE_CHUNKS):
+            if step + 3 < len(LATE_CHUNKS) - 1:
                 late_chunk(step + 3)
+            if step == 3:
+                round_and_weave(nc, res_woven[:], res_pairs[-1][:, :, TILE:PAIR])
             if step == 1:
                 deal_down_weights()
             if step >= 1 and step < last:
@@ -353,13 +394,16 @@ def tile_list_tanh_mix_resP_kernel(
         down_half(7, 1)
         hand_on_stage(4)
         hand_on_stage(5)
-        store_scales(0, J - PAIR, nc.sync)
         hand_on_stage(6)
         s, side = divmod(last, 2)
-        for j0 in (0, TILE // 2):
-            add_residual(last, j0, TILE // 2)
+        last_woven = ring.tile([P, TILE, PACK], BF16, name="out_woven", tag="out_woven", align_bytes=64)
+        nc.vector.tensor_tensor(last_woven[:], sums[last][:].rearrange("p i j -> p j i"), res_woven[:], ADD)
+        add_residual(last, 0, TILE)
         store_rows(last)
-        for j0 in (0, TILE // 2):
-            hand_on(out_pairs[s][:, :, side * TILE + j0 : side * TILE + j0 + TILE // 2], last * TILE + j0, TILE // 2)
+        nc.vector.quantize_mx(
+            out=out_codes[:, last * TILE : J].bitcast(E4M3),
+            scales=out_scales[:, last * TILE : J],
+            in_=last_woven[:].rearrange("p j t -> p (j t)"),
+        )
         store_planes(s * PAIR, PAIR)
-        store_scales(J - PAIR, PAIR, nc.scalar)
+        store_scales(0, J, nc.sync)

@@ -15,27 +15,41 @@ E4M3 = mybir.dt.float8_e4m3fn_x4
 E2M1 = mybir.dt.float4_e2m1fn_x4
 MULT = mybir.AluOpType.mult
 ADD = mybir.AluOpType.add
+COPY = mybir.ActivationFunctionType.Copy
 TANH = mybir.ActivationFunctionType.Tanh
 
 P = 128
 PACK = 4
 PASS = P * PACK
+GROUP = 16
+QUADRANT = 32
 TILE = 128
 TILES = J // TILE
-LATE_CHUNKS = (128, 128, 128, 128, 256, 256)
+LAST = TILES - 1
 PAIR = 2 * TILE
 HALF = J // 2
-GATES_FIRST = 8
-LENT = {(2, 1): 0, (3, 0): 1, (3, 1): 2, (4, 0): 3}
+
 BANKS = {"ga": 3, "ub": 3, "turned": 1, "y": 1}
-HOLD = 4
+
+PICKS_AT_ONCE = 2
+PICKS_AFTER_QUANTISE = 3
+FIRST_LENDING_UNIT = 6
 
 
-def round_and_weave(nc, woven, planes):
-    nc.scalar.copy(
-        out=woven.rearrange("p (c i) t -> p c t i", i=4),
-        in_=planes.rearrange("p t (c i) -> p c t i", i=4),
+def weave(nc, woven, planes):
+    nc.scalar.activation(
+        out=woven.rearrange("p (c e) i -> p c i e", e=4),
+        in_=planes.rearrange("p i (c e) -> p c i e", e=4),
+        func=COPY,
     )
+
+
+def in_pair_order(rows):
+    return rows.rearrange("j (u p e) -> j u p e", u=2, e=2)
+
+
+def from_r_order(rows):
+    return rows.rearrange("j (p u e) -> j u p e", u=2, e=2)
 
 
 def tile_list_tanh_mix_resP_kernel(
@@ -53,43 +67,40 @@ def tile_list_tanh_mix_resP_kernel(
         ring = ctx.enter_context(tc.tile_pool(name="ring", bufs=2))
         psum = ctx.enter_context(tc.psum_pool(name="psum", bufs=1))
 
-        offsets = keep.tile([P, J // 16], U16, name="offsets")
+        def bank(shape, tag):
+            return psum.tile(shape, F32, name=tag, tag=tag, bufs=BANKS[tag])
+
+        offsets = keep.tile([P, J // GROUP], U16, name="offsets")
         nc.sync.dma_start(offsets[:], offs)
 
-        up_planes = keep.tile([P, 2 * R], U8, name="up_planes", align_bytes=64)
-        down_planes_raw = keep.tile([P, N], U8, name="down_planes_raw", align_bytes=64)
-        nc.vector.memset(up_planes[:].bitcast(I32), 0)
-        nc.vector.memset(down_planes_raw[:].bitcast(I32), 0)
+        first_scales = keep.tile([P, 2 * R], U8, name="first_scales", align_bytes=64)
+        second_scales_raw = keep.tile([P, N], U8, name="second_scales_raw", align_bytes=64)
+        nc.vector.memset(first_scales[:].bitcast(I32), 0)
+        nc.vector.memset(second_scales_raw[:].bitcast(I32), 0)
         ident = keep.tile([P, P], F32, name="ident")
         make_identity(nc, ident[:])
-        warm = keep.tile([P, 2], F32, name="warm")
-        nc.vector.memset(warm[:, 0:1], 0.0)
-        nc.scalar.activation(out=warm[:, 1:2], in_=warm[:, 0:1], func=TANH)
 
         wd8_raw = keep.tile([P, N], I32, name="wd8_raw")
         wd4_raw = keep.tile([P, 2 * N], U8, name="wd4_raw")
-
         x_planes = [[keep.tile([P, T], F32, name="x_%d_%d" % (a, i)) for i in range(PACK)] for a in range(2)]
         weights = keep.tile([P, J], F32, name="weights")
         wg = [keep.tile([P, R], I32, name="wg_%d" % a, align_bytes=64) for a in range(2)]
         wu = [keep.tile([P, 2 * R], U8, name="wu_%d" % a, align_bytes=64) for a in range(2)]
-
-        def load_up_planes(q):
-            nc.sync.dma_start(
-                up_planes[32 * q : 32 * q + 4, :].bitcast(I32).rearrange("r (a n) -> r a n", a=2),
-                wu_scales[:, 4 * q : 4 * q + 4, :].bitcast(I32).rearrange("a r n -> r a n"),
-            )
-            nc.sync.dma_start(
-                up_planes[32 * q + 4 : 32 * q + 12, 0:R].bitcast(I32),
-                wg_scales[:, 4 * q : 4 * q + 4, :].bitcast(I32),
-            )
-
-        def load_up_words(a):
-            nc.sync.dma_start(wg[a][:], wg_words[a].rearrange("p r i -> p (r i)").bitcast(I32))
-            nc.sync.dma_start(wu[a][:].bitcast(I32), wu_words[a].bitcast(I32))
+        res_pairs = [keep.tile([P, PACK, PAIR], F32, name="res_%d" % s) for s in range(J // PAIR)]
 
         def load_x(a, i):
             nc.sync.dma_start(x_planes[a][i][:], x_rows[a, i])
+
+        def load_first_scales(q):
+            row = QUADRANT * q
+            nc.sync.dma_start(
+                first_scales[row : row + 4, :].bitcast(I32).rearrange("r (a n) -> r a n", a=2),
+                wu_scales[:, 4 * q : 4 * q + 4, :].bitcast(I32).rearrange("a r n -> r a n"),
+            )
+            nc.sync.dma_start(
+                first_scales[row + 4 : row + 12, 0:R].bitcast(I32),
+                wg_scales[:, 4 * q : 4 * q + 4, :].bitcast(I32),
+            )
 
         def load_wg(a):
             nc.sync.dma_start(wg[a][:], wg_words[a].rearrange("p r i -> p (r i)").bitcast(I32))
@@ -97,313 +108,261 @@ def tile_list_tanh_mix_resP_kernel(
         def load_wu(a):
             nc.sync.dma_start(wu[a][:].bitcast(I32), wu_words[a].bitcast(I32))
 
+        def load_res(s):
+            nc.sync.dma_start(res_pairs[s][:], res_rows[:, :, s * PAIR : (s + 1) * PAIR])
+
         load_x(0, 0)
-        for s in range(2):
-            nc.sync.dma_start(weights[:, s * HALF : (s + 1) * HALF], wgt[:, s * HALF : (s + 1) * HALF])
+        nc.sync.dma_start(weights[:, 0:PAIR], wgt[:, 0:PAIR])
+        nc.sync.dma_start(weights[:, PAIR:J], wgt[:, PAIR:J])
         for i in range(1, PACK):
             load_x(0, i)
         for i in range(PACK - 1):
-            load_up_planes(i)
+            load_first_scales(i)
             load_x(1, i)
-        load_up_planes(PACK - 1)
+        load_first_scales(PACK - 1)
         load_wg(0)
-        load_x(1, 3)
+        load_x(1, PACK - 1)
         load_wu(0)
         load_wg(1)
         load_wu(1)
-        def load_down():
-            nc.sync.dma_start(wd8_raw[:], wd8_words[0].rearrange("p n i -> p (n i)").bitcast(I32))
-            nc.sync.dma_start(wd4_raw[:].bitcast(I32), wd4_words[0].bitcast(I32))
-            for q in range(4):
-                nc.sync.dma_start(
-                    down_planes_raw[32 * q : 32 * q + 4, :].bitcast(I32),
-                    wd4_scales[0, 4 * q : 4 * q + 4, :].bitcast(I32),
-                )
-                nc.sync.dma_start(
-                    down_planes_raw[32 * q + 4 : 32 * q + 8, :].bitcast(I32),
-                    wd8_scales[0, 4 * q : 4 * q + 4, :].bitcast(I32),
-                )
-
-        res_pairs = [keep.tile([P, PACK, PAIR], F32, name="res_%d" % s) for s in range(J // PAIR)]
-        for s in range(J // PAIR):
-            nc.sync.dma_start(res_pairs[s][:], res_rows[:, :, s * PAIR : (s + 1) * PAIR])
-            if s == 1:
-                load_down()
+        load_res(0)
+        load_res(1)
+        nc.sync.dma_start(wd8_raw[:], wd8_words[0].rearrange("p n i -> p (n i)").bitcast(I32))
+        nc.sync.dma_start(wd4_raw[:].bitcast(I32), wd4_words[0].bitcast(I32))
+        for q in range(P // QUADRANT):
+            row = QUADRANT * q
+            nc.sync.dma_start(
+                second_scales_raw[row : row + 4, :].bitcast(I32),
+                wd4_scales[0, 4 * q : 4 * q + 4, :].bitcast(I32),
+            )
+            nc.sync.dma_start(
+                second_scales_raw[row + 4 : row + 8, :].bitcast(I32),
+                wd8_scales[0, 4 * q : 4 * q + 4, :].bitcast(I32),
+            )
+        load_res(2)
+        load_res(3)
 
         wd8 = keep.tile([P, N], I32, name="wd8", align_bytes=64)
         wd4 = keep.tile([P, 2 * N], U8, name="wd4", align_bytes=64)
-        down_planes = keep.tile([P, N], U8, name="down_planes", align_bytes=64)
+        second_scales = keep.tile([P, N], U8, name="second_scales", align_bytes=64)
         xg_codes = [keep.tile([P, J], I32, name="xg_codes_%d" % a, align_bytes=64) for a in range(2)]
         xg_scales = [keep.tile([P, J], U8, name="xg_scales_%d" % a, align_bytes=64) for a in range(2)]
 
-        def pick(picked, a, i, j0, width):
+        def pick(row, a, i, j0, j1):
             nc.vector.tensor_tensor(
-                picked[:, i, :],
-                x_planes[a][i][:].indirect(offsets[:, j0 // 16 : (j0 + width) // 16]),
-                weights[:, j0 : j0 + width],
+                row,
+                x_planes[a][i][:].indirect(offsets[:, j0 // GROUP : j1 // GROUP]),
+                weights[:, j0:j1],
                 MULT,
             )
 
-        def quantise_picks(planes, a, j0, width, tag):
-            woven = ring.tile([P, width, PACK], BF16, name=tag, tag=tag, align_bytes=64)
-            round_and_weave(nc, woven[:], planes)
+        def woven_tile(width, tag):
+            return ring.tile([P, width, PACK], BF16, name=tag, tag=tag, align_bytes=64)
+
+        def quantise(codes, scales, woven):
             nc.vector.quantize_mx(
-                out=xg_codes[a][:, j0 : j0 + width].bitcast(E4M3),
-                scales=xg_scales[a][:, j0 : j0 + width],
-                in_=woven[:].rearrange("p j t -> p (j t)"),
+                out=codes.bitcast(E4M3), scales=scales, in_=woven.rearrange("p j i -> p (j i)")
             )
+
+        def quantise_picks(planes, woven, a, j0, j1):
+            weave(nc, woven, planes)
+            quantise(xg_codes[a][:, j0:j1], xg_scales[a][:, j0:j1], woven)
 
         early = keep.tile([P, PACK, J], F32, name="early")
         for i in range(PACK):
-            for j0 in ((0, HALF) if i in (0, PACK - 1) else (0,)):
-                width = HALF if i in (0, PACK - 1) else J
-                pick(early[:, :, j0 : j0 + width], 0, i, j0, width)
-        for s in range(2):
-            quantise_picks(early[:, :, s * HALF : (s + 1) * HALF], 0, s * HALF, HALF, "woven_early")
+            cuts = {0: (0, PAIR, J), PACK - 1: (0, HALF, J)}.get(i, (0, J))
+            for j0, j1 in zip(cuts, cuts[1:]):
+                pick(early[:, i, j0:j1], 0, i, j0, j1)
+        for j0 in (0, HALF):
+            quantise_picks(early[:, :, j0 : j0 + HALF], woven_tile(HALF, "woven_early")[:], 0, j0, j0 + HALF)
 
-        late_first = keep.tile([P, PACK, HALF], F32, name="late_first")
-        late_next = keep.tile([P, PACK + 1, PAIR], F32, name="late_next", align_bytes=64)
-        late_last = keep.tile([P, PACK, PASS], F32, name="late_last")
-        late = [late_first[:, :, c * TILE : (c + 1) * TILE] for c in range(HOLD)]
-        late.extend([late_next, late_last[:, :, 0:PAIR]])
+        late = keep.tile([P, PACK, HALF], F32, name="late")
+        deferred = keep.tile([P, 2 * PACK, PASS], F32, name="deferred", align_bytes=64)
+
+        def deferred_pick(n):
+            s, i = divmod(n, PACK)
+            j0 = HALF + s * PAIR
+            pick(deferred[:, n, 0:PAIR], 1, i, j0, j0 + PAIR)
+            if i == PACK - 1:
+                planes = deferred[:, s * PACK : (s + 1) * PACK, 0:PAIR]
+                quantise_picks(planes, woven_tile(PAIR, "woven_late")[:], 1, j0, j0 + PAIR)
+
         for i in range(PACK - 1):
-            pick(late_first, 1, i, 0, HALF)
-            pick(late_next, 1, i, HALF, PAIR)
+            pick(late[:, i, :], 1, i, 0, HALF)
+            if i < PICKS_AT_ONCE:
+                deferred_pick(i)
 
-        def late_pick(c):
-            pick(late[c], 1, PACK - 1, sum(LATE_CHUNKS[:c]), LATE_CHUNKS[c])
-
-        def late_chunk(c):
-            j0, width = sum(LATE_CHUNKS[:c]), LATE_CHUNKS[c]
-            if c + HOLD < len(LATE_CHUNKS) - 1:
-                room = late[c + HOLD][:, PACK - 1 :, :].rearrange("p t j -> p (t j)").bitcast(BF16)
-                woven = room[:, 0 : PACK * width].rearrange("p (j t) -> p j t", t=PACK)
+        def quantise_late(jt):
+            j0, j1 = jt * TILE, (jt + 1) * TILE
+            if jt < PICKS_AFTER_QUANTISE:
+                n = PICKS_AT_ONCE + jt
+                woven = deferred[:, n, 0:PAIR].bitcast(BF16).rearrange("p (j i) -> p j i", i=PACK)
+                quantise_picks(late[:, :, j0:j1], woven, 1, j0, j1)
+                deferred_pick(n)
             else:
-                spare = ring.tile([P, width, PACK], BF16, name="woven_late", tag="woven_late", align_bytes=64)
-                woven = spare[:]
-            round_and_weave(nc, woven, late[c][:, 0:PACK, :])
-            nc.vector.quantize_mx(
-                out=xg_codes[1][:, j0 : j0 + width].bitcast(E4M3),
-                scales=xg_scales[1][:, j0 : j0 + width],
-                in_=woven.rearrange("p j t -> p (j t)"),
-            )
-            if c + HOLD < len(LATE_CHUNKS) - 1:
-                late_pick(c + HOLD)
+                quantise_picks(late[:, :, j0:j1], woven_tile(TILE, "woven_late")[:], 1, j0, j1)
 
-        hidden = {}
+        h_rows = {}
 
-        gates = {}
-
-        def gate_unit(jt, b):
+        def first_stage(jt, b):
             cols = slice(jt * TILE, (jt + 1) * TILE)
-            tag = "turned" if (jt, b) == (1, 1) else "ga"
-            ga = psum.tile([P, PASS], F32, name="ga", tag=tag, bufs=BANKS[tag])
+            unit = 2 * jt + b
+            ga_tag, ub_tag = ("turned", "y") if unit == BANKS["ga"] else ("ga", "ub")
+            ga = bank([P, PASS], ga_tag)
             for a in range(2):
                 nc.tensor.matmul_mx(
                     out=ga[:],
                     lhsT=xg_codes[a][:, cols].bitcast(E4M3),
                     lhsT_scale=xg_scales[a][:, cols],
                     rhs=wg[a][:, b * PASS : (b + 1) * PASS].bitcast(E4M3),
-                    rhs_scale=up_planes[4 + 4 * a : P, b * PASS : (b + 1) * PASS],
+                    rhs_scale=first_scales[4 + 4 * a : P, b * PASS : (b + 1) * PASS],
                     start=(a == 0),
                     stop=(a == 1),
                 )
-            if (jt, b) in LENT:
-                gate = late_last[:, LENT[jt, b], :]
+            n = PICKS_AT_ONCE + PICKS_AFTER_QUANTISE + unit - FIRST_LENDING_UNIT
+            lends = unit >= FIRST_LENDING_UNIT and n < 2 * PACK
+            if lends:
+                gate = deferred[:, n, :]
             else:
-                gate = ring.tile([P, PASS], F32, name="gate", tag="gate", bufs=3)
-            nc.scalar.activation(
-                out=gate[:].rearrange("j (u p e) -> j u p e", u=2, e=2),
-                in_=ga[:].rearrange("j (p u e) -> j u p e", u=2, e=2),
-                func=TANH,
-            )
-            gates[jt, b] = gate
-
-        def up_unit(jt, b):
-            cols = slice(jt * TILE, (jt + 1) * TILE)
-            tag = "y" if (jt, b) == (1, 1) else "ub"
-            ub = psum.tile([P, PASS], F32, name="ub", tag=tag, bufs=BANKS[tag])
+                gate = ring.tile([P, PASS], F32, name="gate", tag="gate", bufs=3)[:]
+            nc.scalar.activation(out=in_pair_order(gate), in_=from_r_order(ga[:]), func=TANH)
+            ub = bank([P, PASS], ub_tag)
             for a in range(2):
                 nc.tensor.matmul_mx(
                     out=ub[:],
                     lhsT=xg_codes[a][:, cols].bitcast(E4M3),
                     lhsT_scale=xg_scales[a][:, cols],
                     rhs=wu[a][:, 2 * b * PASS : 2 * (b + 1) * PASS].bitcast(E2M1),
-                    rhs_scale=up_planes[:, a * R + b * PASS : a * R + (b + 1) * PASS],
+                    rhs_scale=first_scales[:, a * R + b * PASS : a * R + (b + 1) * PASS],
                     start=(a == 0),
                     stop=(a == 1),
                 )
-            h_rows = ring.tile([P, PASS], BF16, name="h_rows", tag="h_rows", bufs=6)
+            h_rows[jt, b] = ring.tile([P, PASS], BF16, name="h_rows", tag="h_rows", bufs=6)
             nc.vector.tensor_tensor(
-                h_rows[:].rearrange("j (u p e) -> j u p e", u=2, e=2),
-                ub[:].rearrange("j (p u e) -> j u p e", u=2, e=2),
-                gates[jt, b][:].rearrange("j (u p e) -> j u p e", u=2, e=2),
-                MULT,
+                in_pair_order(h_rows[jt, b][:]), from_r_order(ub[:]), in_pair_order(gate), MULT
             )
-            hidden[jt, b] = h_rows
-            if (jt, b) in LENT:
-                pick(late[-1], 1, LENT[jt, b], J - LATE_CHUNKS[-1], LATE_CHUNKS[-1])
-                if LENT[jt, b] == PACK - 1:
-                    late_chunk(len(LATE_CHUNKS) - 1)
+            if lends:
+                deferred_pick(n)
 
-        def up_stage(jt):
-            if jt >= GATES_FIRST:
-                for unit in (gate_unit, up_unit):
-                    for b in range(2):
-                        unit(jt, b)
-            else:
-                for b in range(2):
-                    gate_unit(jt, b)
-                    up_unit(jt, b)
+        h_operand = {}
 
-        h_quantised = {}
-
-        def turn_stage(jt, halves=(0, 1), tag="turned"):
+        def turn(jt, halves, tag):
             count = len(halves)
-            turned = psum.tile([P, count, 2, TILE], F32, name="turned", tag=tag, bufs=BANKS[tag])
-            for n, b in enumerate(halves):
-                pairs = hidden[jt, b][:].bitcast(F32)
+            turned = bank([P, count, 2, TILE], tag)
+            for m, b in enumerate(halves):
+                words = h_rows[jt, b][:].bitcast(F32)
                 for u in range(2):
-                    nc.tensor.transpose(turned[:, n, u, :], pairs[:, u * P : (u + 1) * P], ident[:])
+                    nc.tensor.transpose(turned[:, m, u, :], words[:, u * P : (u + 1) * P], ident[:])
             h_woven = ring.tile([P, count * TILE * PACK], BF16, name="h_woven", tag="h_woven", bufs=3, align_bytes=64)
             nc.scalar.copy(
-                out=h_woven[:].bitcast(F32).rearrange("p (b j u) -> p b j u", b=count, u=2),
-                in_=turned[:].rearrange("p b u j -> p b j u"),
+                out=h_woven[:].bitcast(F32).rearrange("p (m j u) -> p m j u", m=count, u=2),
+                in_=turned[:].rearrange("p m u j -> p m j u"),
             )
             h_codes = ring.tile([P, count * TILE], I32, name="h_codes", tag="h_codes", bufs=4, align_bytes=64)
             h_scales = ring.tile([P, count * TILE], U8, name="h_scales", tag="h_scales", bufs=4, align_bytes=64)
             nc.vector.quantize_mx(out=h_codes[:].bitcast(E4M3), scales=h_scales[:], in_=h_woven[:])
-            for n, b in enumerate(halves):
-                h_quantised[jt, b] = (h_codes[:, n * TILE : (n + 1) * TILE], h_scales[:, n * TILE : (n + 1) * TILE])
+            for m, b in enumerate(halves):
+                cols = slice(m * TILE, (m + 1) * TILE)
+                h_operand[jt, b] = (h_codes[:, cols], h_scales[:, cols])
 
         out_codes = keep.tile([P, J], I32, name="out_codes", align_bytes=64)
         out_scales = keep.tile([P, J], U8, name="out_scales", align_bytes=64)
         out_pairs = [keep.tile([P, PACK, PAIR], F32, name="out_%d" % s) for s in range(J // PAIR)]
 
-        def deal_down_weights():
-            nc.vector.tensor_copy(
-                out=wd8[:].rearrange("p (i m) -> p i m", i=PACK),
-                in_=wd8_raw[:].rearrange("p (m i) -> p i m", i=PACK),
-            )
-            nc.vector.tensor_copy(
-                out=wd4[:].bitcast(U16).rearrange("p (i m) -> p i m", i=PACK),
-                in_=wd4_raw[:].bitcast(U16).rearrange("p (m i) -> p i m", i=PACK),
-            )
-            nc.vector.tensor_copy(
-                out=down_planes[:].rearrange("p (i m) -> p i m", i=PACK),
-                in_=down_planes_raw[:].rearrange("p (m i) -> p i m", i=PACK),
-            )
+        def deal_second_weights():
+            for dealt, raw in (
+                (wd8[:], wd8_raw[:]),
+                (wd4[:].bitcast(U16), wd4_raw[:].bitcast(U16)),
+                (second_scales[:], second_scales_raw[:]),
+            ):
+                nc.vector.tensor_copy(
+                    out=dealt.rearrange("p (i m) -> p i m", i=PACK),
+                    in_=raw.rearrange("p (m i) -> p i m", i=PACK),
+                )
 
-        def hand_on(planes, j0, width):
-            out_woven = ring.tile([P, width, PACK], BF16, name="out_woven", tag="out_woven", align_bytes=64)
-            round_and_weave(nc, out_woven[:], planes)
-            nc.vector.quantize_mx(
-                out=out_codes[:, j0 : j0 + width].bitcast(E4M3),
-                scales=out_scales[:, j0 : j0 + width],
-                in_=out_woven[:].rearrange("p j t -> p (j t)"),
-            )
+        def second_stage(jt, tag):
+            y = bank([P, PACK, TILE], tag)
+            for b in range(2):
+                codes, scales = h_operand[jt, b]
+                for i in range(PACK):
+                    if b == 0:
+                        lhsT = wd8[:, i * P : (i + 1) * P].bitcast(E4M3)
+                        lhsT_scale = second_scales[4:P, i * P : (i + 1) * P]
+                    else:
+                        lhsT = wd4[:, 2 * i * P : 2 * (i + 1) * P].bitcast(E2M1)
+                        lhsT_scale = second_scales[:, i * P : (i + 1) * P]
+                    nc.tensor.matmul_mx(
+                        out=y[:, i, :],
+                        lhsT=lhsT,
+                        lhsT_scale=lhsT_scale,
+                        rhs=codes.bitcast(E4M3),
+                        rhs_scale=scales,
+                        start=(b == 0 and i == 0),
+                        stop=(b == 1 and i == PACK - 1),
+                    )
+            return y
 
-        sums = {}
-
-        def down_pass(jt, b, i, start, stop):
-            codes, scales = h_quantised[jt, b]
-            if b == 0:
-                lhsT = wd8[:, i * P : (i + 1) * P].bitcast(E4M3)
-                lhsT_scale = down_planes[4:P, i * P : (i + 1) * P]
-            else:
-                lhsT = wd4[:, 2 * i * P : 2 * (i + 1) * P].bitcast(E2M1)
-                lhsT_scale = down_planes[:, i * P : (i + 1) * P]
-            nc.tensor.matmul_mx(
-                out=sums[jt][:, i, :], lhsT=lhsT, lhsT_scale=lhsT_scale,
-                rhs=codes.bitcast(E4M3), rhs_scale=scales, start=start, stop=stop,
-            )
-
-        def down_half(jt, b, tag="y"):
-            if b == 0:
-                sums[jt] = psum.tile([P, PACK, TILE], F32, name="y", tag=tag, bufs=BANKS[tag])
-            for i in range(PACK):
-                down_pass(jt, b, i, b == 0 and i == 0, b == 1 and i == PACK - 1)
-
-        def add_residual(jt, j0, width):
+        def of_tile(pairs, jt):
             s, side = divmod(jt, 2)
-            part = slice(side * TILE + j0, side * TILE + j0 + width)
-            nc.vector.tensor_tensor(
-                out_pairs[s][:, :, part], sums[jt][:, :, j0 : j0 + width], res_pairs[s][:, :, part], ADD
-            )
+            return pairs[s][:, :, side * TILE : (side + 1) * TILE]
 
-        def store_rows(jt):
+        def add_and_store(jt, y):
+            nc.vector.tensor_tensor(of_tile(out_pairs, jt), y[:], of_tile(res_pairs, jt), ADD)
             s, side = divmod(jt, 2)
-            part = slice(side * TILE, (side + 1) * TILE)
-            if s == J // PAIR - 1:
-                nc.sync.dma_start(out_rows[:, :, jt * TILE : (jt + 1) * TILE], out_pairs[s][:, :, part])
+            if jt >= LAST - 1:
+                nc.sync.dma_start(out_rows[:, :, jt * TILE : (jt + 1) * TILE], of_tile(out_pairs, jt))
             elif side == 1:
                 nc.sync.dma_start(out_rows[:, :, s * PAIR : (s + 1) * PAIR], out_pairs[s][:])
 
-        def down_stage(jt, tag="y"):
-            down_half(jt, 0, tag)
-            down_half(jt, 1)
-            add_residual(jt, 0, TILE)
-            store_rows(jt)
+        def hand_on(jt, woven):
+            cols = slice(jt * TILE, (jt + 1) * TILE)
+            quantise(out_codes[:, cols], out_scales[:, cols], woven)
+            if jt % 2 == 1:
+                both = slice((jt - 1) * TILE, (jt + 1) * TILE)
+                nc.sync.dma_start(out_words[:, both], out_codes[:, both])
 
-        def store_planes(j0, width):
-            nc.sync.dma_start(out_words[:, j0 : j0 + width], out_codes[:, j0 : j0 + width])
+        def weave_and_hand_on(jt):
+            woven = woven_tile(TILE, "woven_out")[:]
+            weave(nc, woven, of_tile(out_pairs, jt))
+            hand_on(jt, woven)
 
-        def store_scales(j0, width, queue):
-            for q in range(4):
-                queue.dma_start(
-                    out_2[0, 4 * q : 4 * q + 4, j0 : j0 + width].bitcast(I32),
-                    out_scales[32 * q : 32 * q + 4, j0 : j0 + width].bitcast(I32),
-                )
+        for jt in range(TILES // 2):
+            pick(late[:, PACK - 1, jt * TILE : (jt + 1) * TILE], 1, PACK - 1, jt * TILE, (jt + 1) * TILE)
+        for jt in range(TILES // 2 - 1):
+            quantise_late(jt)
 
-        def hand_on_stage(jt):
-            s, side = divmod(jt, 2)
-            part = slice(side * TILE, (side + 1) * TILE)
-            if s >= 2:
-                hand_on(out_pairs[s][:, :, part], jt * TILE, TILE)
-            elif side == 1:
-                hand_on(out_pairs[s][:], s * PAIR, PAIR)
-            if side == 1:
-                store_planes(s * PAIR, PAIR)
-
-        for c in range(HOLD):
-            late_pick(c)
-        for c in range(3):
-            late_chunk(c)
-        last = TILES - 1
         res_woven = keep.tile([P, TILE, PACK], F32, name="res_woven")
-        for step in range(TILES):
-            up_stage(step)
-            if step + 3 < len(LATE_CHUNKS) - 1:
-                late_chunk(step + 3)
-            if step == 3:
-                round_and_weave(nc, res_woven[:], res_pairs[-1][:, :, TILE:PAIR])
+        for step in range(LAST):
+            first_stage(step, 0)
+            first_stage(step, 1)
+            if step == 0:
+                quantise_late(TILES // 2 - 1)
             if step == 1:
-                deal_down_weights()
-            if step >= 1 and step < last:
-                turn_stage(step - 1)
-            if step >= 2 and step < last:
-                down_stage(step - 2)
-            if step >= 3 and step < last:
-                hand_on_stage(step - 3)
-        turn_stage(6)
-        turn_stage(7, (0,), "ga")
-        turn_stage(7, (1,), "ub")
-        down_stage(5)
-        down_stage(6, "ga")
-        down_half(7, 0, "ub")
-        down_half(7, 1)
-        hand_on_stage(4)
-        hand_on_stage(5)
-        hand_on_stage(6)
-        s, side = divmod(last, 2)
-        last_woven = ring.tile([P, TILE, PACK], BF16, name="out_woven", tag="out_woven", align_bytes=64)
-        nc.vector.tensor_tensor(last_woven[:], sums[last][:].rearrange("p i j -> p j i"), res_woven[:], ADD)
-        add_residual(last, 0, TILE)
-        store_rows(last)
-        nc.vector.quantize_mx(
-            out=out_codes[:, last * TILE : J].bitcast(E4M3),
-            scales=out_scales[:, last * TILE : J],
-            in_=last_woven[:].rearrange("p j t -> p (j t)"),
-        )
-        store_planes(s * PAIR, PAIR)
-        store_scales(0, J, nc.sync)
+                deal_second_weights()
+            if step >= 1:
+                turn(step - 1, (0, 1), "turned")
+            if step >= 2:
+                add_and_store(step - 2, second_stage(step - 2, "y"))
+            if step >= 3:
+                weave_and_hand_on(step - 3)
+        weave(nc, res_woven[:], of_tile(res_pairs, LAST))
+
+        first_stage(LAST, 0)
+        first_stage(LAST, 1)
+        turn(LAST - 1, (0, 1), "turned")
+        turn(LAST, (0,), "ga")
+        turn(LAST, (1,), "ub")
+        add_and_store(LAST - 2, second_stage(LAST - 2, "y"))
+        add_and_store(LAST - 1, second_stage(LAST - 1, "ga"))
+        y_last = second_stage(LAST, "ub")
+        for jt in range(LAST - 3, LAST):
+            weave_and_hand_on(jt)
+        last_woven = keep.tile([P, TILE, PACK], BF16, name="last_woven", align_bytes=64)
+        nc.vector.tensor_tensor(last_woven[:], y_last[:].rearrange("p i j -> p j i"), res_woven[:], ADD)
+        add_and_store(LAST, y_last)
+        hand_on(LAST, last_woven[:])
+        for q in range(P // QUADRANT):
+            nc.sync.dma_start(
+                out_2[0, 4 * q : 4 * q + 4, :].bitcast(I32),
+                out_scales[QUADRANT * q : QUADRANT * q + 4, :].bitcast(I32),
+            )

@@ -23,6 +23,8 @@ PACK = 4
 PASS = P * PACK
 GROUP = 16
 QUADRANT = 32
+ROWS = 4
+BLOCKS = PASS // 32
 TILE = 128
 TILES = J // TILE
 LAST = TILES - 1
@@ -92,14 +94,13 @@ def tile_list_tanh_mix_resP_kernel(
             nc.sync.dma_start(x_planes[a][i][:], x_rows[a, i])
 
         def load_first_scales(q):
-            row = QUADRANT * q
             nc.sync.dma_start(
-                first_scales[row : row + 4, :].bitcast(I32).rearrange("r (a n) -> r a n", a=2),
-                wu_scales[:, 4 * q : 4 * q + 4, :].bitcast(I32).rearrange("a r n -> r a n"),
+                first_scales[q:P:QUADRANT, :].bitcast(I32).rearrange("r (a n) -> r a n", a=2),
+                wu_scales[:, q:BLOCKS:ROWS, :].bitcast(I32).rearrange("a r n -> r a n"),
             )
             nc.sync.dma_start(
-                first_scales[row + 4 : row + 12, 0:R].bitcast(I32),
-                wg_scales[:, 4 * q : 4 * q + 4, :].bitcast(I32),
+                first_scales[QUADRANT * q + ROWS : QUADRANT * q + 3 * ROWS, 0:R].bitcast(I32),
+                wg_scales[:, ROWS * q : ROWS * (q + 1), :].bitcast(I32),
             )
 
         def load_wg(a):
@@ -119,7 +120,7 @@ def tile_list_tanh_mix_resP_kernel(
         for i in range(PACK - 1):
             load_first_scales(i)
             load_x(1, i)
-        load_first_scales(PACK - 1)
+        load_first_scales(ROWS - 1)
         load_wg(0)
         load_x(1, PACK - 1)
         load_wu(0)
@@ -129,15 +130,14 @@ def tile_list_tanh_mix_resP_kernel(
         load_res(1)
         nc.sync.dma_start(wd8_raw[:], wd8_words[0].rearrange("p n i -> p (n i)").bitcast(I32))
         nc.sync.dma_start(wd4_raw[:].bitcast(I32), wd4_words[0].bitcast(I32))
-        for q in range(P // QUADRANT):
-            row = QUADRANT * q
+        for q in range(ROWS):
             nc.sync.dma_start(
-                second_scales_raw[row : row + 4, :].bitcast(I32),
-                wd4_scales[0, 4 * q : 4 * q + 4, :].bitcast(I32),
+                second_scales_raw[q:P:QUADRANT, :].bitcast(I32),
+                wd4_scales[0, q:BLOCKS:ROWS, :].bitcast(I32),
             )
             nc.sync.dma_start(
-                second_scales_raw[row + 4 : row + 8, :].bitcast(I32),
-                wd8_scales[0, 4 * q : 4 * q + 4, :].bitcast(I32),
+                second_scales_raw[ROWS + q : P : QUADRANT, :].bitcast(I32),
+                wd8_scales[0, q:BLOCKS:ROWS, :].bitcast(I32),
             )
         load_res(2)
         load_res(3)
@@ -215,7 +215,7 @@ def tile_list_tanh_mix_resP_kernel(
                     lhsT=xg_codes[a][:, cols].bitcast(E4M3),
                     lhsT_scale=xg_scales[a][:, cols],
                     rhs=wg[a][:, b * PASS : (b + 1) * PASS].bitcast(E4M3),
-                    rhs_scale=first_scales[4 + 4 * a : P, b * PASS : (b + 1) * PASS],
+                    rhs_scale=first_scales[ROWS * (1 + a) : P, b * PASS : (b + 1) * PASS],
                     start=(a == 0),
                     stop=(a == 1),
                 )
@@ -287,7 +287,7 @@ def tile_list_tanh_mix_resP_kernel(
                 for i in range(PACK):
                     if b == 0:
                         lhsT = wd8[:, i * P : (i + 1) * P].bitcast(E4M3)
-                        lhsT_scale = second_scales[4:P, i * P : (i + 1) * P]
+                        lhsT_scale = second_scales[ROWS:P, i * P : (i + 1) * P]
                     else:
                         lhsT = wd4[:, 2 * i * P : 2 * (i + 1) * P].bitcast(E2M1)
                         lhsT_scale = second_scales[:, i * P : (i + 1) * P]
@@ -361,8 +361,8 @@ def tile_list_tanh_mix_resP_kernel(
         nc.vector.tensor_tensor(last_woven[:], y_last[:].rearrange("p i j -> p j i"), res_woven[:], ADD)
         add_and_store(LAST, y_last)
         hand_on(LAST, last_woven[:])
-        for q in range(P // QUADRANT):
-            nc.sync.dma_start(
-                out_2[0, 4 * q : 4 * q + 4, :].bitcast(I32),
-                out_scales[QUADRANT * q : QUADRANT * q + 4, :].bitcast(I32),
+        for q in range(ROWS):
+            nc.scalar.dma_start(
+                out_2[0, q:BLOCKS:ROWS, :].bitcast(I32),
+                out_scales[q:P:QUADRANT, :].bitcast(I32),
             )

from contextlib import ExitStack

import concourse.mybir as mybir
from concourse.masks import make_identity

K, R, N, T, J = 1024, 1024, 512, 2048, 1024
FLOPS = 2 * J * (2 * K * R + R * N)

F32 = mybir.dt.float32
BF16 = mybir.dt.bfloat16
I32 = mybir.dt.int32
U16 = mybir.dt.uint16
U8 = mybir.dt.uint8
E4M3 = mybir.dt.float8_e4m3fn_x4
E2M1 = mybir.dt.float4_e2m1fn_x4
MULT = mybir.AluOpType.mult
ADD = mybir.AluOpType.add
COPY = mybir.ActivationFunctionType.Copy
TANH = mybir.ActivationFunctionType.Tanh

P = 128
PACK = 4
PASS = P * PACK
GROUP = 16
QUADRANT = 32
ROWS = 4
BLOCKS = PASS // 32
TILE = 128
TILES = J // TILE
LAST = TILES - 1
PAIR = 2 * TILE
HALF = J // 2

BANKS = {"ga": 3, "ub": 3, "turned": 1, "y": 1}

PICKS_AT_ONCE = 2
PICKS_AFTER_QUANTISE = 3
FIRST_LENDING_UNIT = 6


def weave(nc, woven, planes):
    nc.scalar.activation(
        out=woven.rearrange("p (c e) i -> p c i e", e=4),
        in_=planes.rearrange("p i (c e) -> p c i e", e=4),
        func=COPY,
    )


def in_pair_order(rows):
    return rows.rearrange("j (u p e) -> j u p e", u=2, e=2)


def from_r_order(rows):
    return rows.rearrange("j (p u e) -> j u p e", u=2, e=2)


def tile_list_tanh_mix_resP_kernel(
    tc, xT, wgt, wg_words, wg_scales, wu_words, wu_scales, wd8_words, wd8_scales,
    wd4_words, wd4_scales, res, offs, out_0, out_1, out_2,
):
    nc = tc.nc
    x_rows = xT.rearrange("(a p i) t -> a i p t", a=2, i=PACK)
    res_rows = res.rearrange("(p i) j -> p i j", i=PACK)
    out_rows = out_0.rearrange("(p i) j -> p i j", i=PACK)
    out_words = out_1[0].rearrange("p j i -> p (j i)").bitcast(I32)

    with ExitStack() as ctx:
        keep = ctx.enter_context(tc.tile_pool(name="keep", bufs=1))
        ring = ctx.enter_context(tc.tile_pool(name="ring", bufs=2))
        psum = ctx.enter_context(tc.psum_pool(name="psum", bufs=1))

        def bank(shape, tag):
            return psum.tile(shape, F32, name=tag, tag=tag, bufs=BANKS[tag])

        offsets = keep.tile([P, J // GROUP], U16, name="offsets")
        nc.sync.dma_start(offsets[:], offs)

        first_scales = keep.tile([P, 2 * R], U8, name="first_scales", align_bytes=64)
        second_scales_raw = keep.tile([P, N], U8, name="second_scales_raw", align_bytes=64)
        nc.vector.memset(first_scales[:].bitcast(I32), 0)
        nc.vector.memset(second_scales_raw[:].bitcast(I32), 0)
        ident = keep.tile([P, P], F32, name="ident")
        make_identity(nc, ident[:])

        wd8_raw = keep.tile([P, N], I32, name="wd8_raw")
        wd4_raw = keep.tile([P, 2 * N], U8, name="wd4_raw")
        x_planes = [[keep.tile([P, T], F32, name="x_%d_%d" % (a, i)) for i in range(PACK)] for a in range(2)]
        weights = keep.tile([P, J], F32, name="weights")
        wg = [keep.tile([P, R], I32, name="wg_%d" % a, align_bytes=64) for a in range(2)]
        wu = [keep.tile([P, 2 * R], U8, name="wu_%d" % a, align_bytes=64) for a in range(2)]
        res_pairs = [keep.tile([P, PACK, PAIR], F32, name="res_%d" % s) for s in range(J // PAIR)]

        def load_x(a, i):
            nc.sync.dma_start(x_planes[a][i][:], x_rows[a, i])

        def load_first_scales(q):
            nc.sync.dma_start(
                first_scales[q:P:QUADRANT, :].bitcast(I32).rearrange("r (a n) -> r a n", a=2),
                wu_scales[:, q:BLOCKS:ROWS, :].bitcast(I32).rearrange("a r n -> r a n"),
            )
            nc.sync.dma_start(
                first_scales[QUADRANT * q + ROWS : QUADRANT * q + 3 * ROWS, 0:R].bitcast(I32),
                wg_scales[:, ROWS * q : ROWS * (q + 1), :].bitcast(I32),
            )

        def load_wg(a):
            nc.sync.dma_start(wg[a][:], wg_words[a].rearrange("p r i -> p (r i)").bitcast(I32))

        def load_wu(a):
            nc.sync.dma_start(wu[a][:].bitcast(I32), wu_words[a].bitcast(I32))

        def load_res(s):
            nc.sync.dma_start(res_pairs[s][:], res_rows[:, :, s * PAIR : (s + 1) * PAIR])

        load_x(0, 0)
        nc.sync.dma_start(weights[:, 0:PAIR], wgt[:, 0:PAIR])
        nc.sync.dma_start(weights[:, PAIR:J], wgt[:, PAIR:J])
        for i in range(1, PACK):
            load_x(0, i)
        for i in range(PACK - 1):
            load_first_scales(i)
            load_x(1, i)
        load_first_scales(ROWS - 1)
        load_wg(0)
        load_x(1, PACK - 1)
        load_wu(0)
        load_wg(1)
        load_wu(1)
        load_res(0)
        load_res(1)
        nc.sync.dma_start(wd8_raw[:], wd8_words[0].rearrange("p n i -> p (n i)").bitcast(I32))
        nc.sync.dma_start(wd4_raw[:].bitcast(I32), wd4_words[0].bitcast(I32))
        for q in range(ROWS):
            nc.sync.dma_start(
                second_scales_raw[q:P:QUADRANT, :].bitcast(I32),
                wd4_scales[0, q:BLOCKS:ROWS, :].bitcast(I32),
            )
            nc.sync.dma_start(
                second_scales_raw[ROWS + q : P : QUADRANT, :].bitcast(I32),
                wd8_scales[0, q:BLOCKS:ROWS, :].bitcast(I32),
            )
        load_res(2)
        load_res(3)

        wd8 = keep.tile([P, N], I32, name="wd8", align_bytes=64)
        wd4 = keep.tile([P, 2 * N], U8, name="wd4", align_bytes=64)
        second_scales = keep.tile([P, N], U8, name="second_scales", align_bytes=64)
        xg_codes = [keep.tile([P, J], I32, name="xg_codes_%d" % a, align_bytes=64) for a in range(2)]
        xg_scales = [keep.tile([P, J], U8, name="xg_scales_%d" % a, align_bytes=64) for a in range(2)]

        def pick(row, a, i, j0, j1):
            nc.vector.tensor_tensor(
                row,
                x_planes[a][i][:].indirect(offsets[:, j0 // GROUP : j1 // GROUP]),
                weights[:, j0:j1],
                MULT,
            )

        def woven_tile(width, tag):
            return ring.tile([P, width, PACK], BF16, name=tag, tag=tag, align_bytes=64)

        def quantise(codes, scales, woven):
            nc.vector.quantize_mx(
                out=codes.bitcast(E4M3), scales=scales, in_=woven.rearrange("p j i -> p (j i)")
            )

        def quantise_picks(planes, woven, a, j0, j1):
            weave(nc, woven, planes)
            quantise(xg_codes[a][:, j0:j1], xg_scales[a][:, j0:j1], woven)

        early = keep.tile([P, PACK, J], F32, name="early")
        for i in range(PACK):
            cuts = {0: (0, PAIR, J), PACK - 1: (0, HALF, J)}.get(i, (0, J))
            for j0, j1 in zip(cuts, cuts[1:]):
                pick(early[:, i, j0:j1], 0, i, j0, j1)
        for j0 in (0, HALF):
            quantise_picks(early[:, :, j0 : j0 + HALF], woven_tile(HALF, "woven_early")[:], 0, j0, j0 + HALF)

        late = keep.tile([P, PACK, HALF], F32, name="late")
        deferred = keep.tile([P, 2 * PACK, PASS], F32, name="deferred", align_bytes=64)

        def deferred_pick(n):
            s, i = divmod(n, PACK)
            j0 = HALF + s * PAIR
            pick(deferred[:, n, 0:PAIR], 1, i, j0, j0 + PAIR)
            if i == PACK - 1:
                planes = deferred[:, s * PACK : (s + 1) * PACK, 0:PAIR]
                quantise_picks(planes, woven_tile(PAIR, "woven_late")[:], 1, j0, j0 + PAIR)

        for i in range(PACK - 1):
            pick(late[:, i, :], 1, i, 0, HALF)
            if i < PICKS_AT_ONCE:
                deferred_pick(i)

        def quantise_late(jt):
            j0, j1 = jt * TILE, (jt + 1) * TILE
            if jt < PICKS_AFTER_QUANTISE:
                n = PICKS_AT_ONCE + jt
                woven = deferred[:, n, 0:PAIR].bitcast(BF16).rearrange("p (j i) -> p j i", i=PACK)
                quantise_picks(late[:, :, j0:j1], woven, 1, j0, j1)
                deferred_pick(n)
            else:
                quantise_picks(late[:, :, j0:j1], woven_tile(TILE, "woven_late")[:], 1, j0, j1)

        h_rows = {}

        def first_stage(jt, b):
            cols = slice(jt * TILE, (jt + 1) * TILE)
            unit = 2 * jt + b
            ga_tag, ub_tag = ("turned", "y") if unit == BANKS["ga"] else ("ga", "ub")
            ga = bank([P, PASS], ga_tag)
            for a in range(2):
                nc.tensor.matmul_mx(
                    out=ga[:],
                    lhsT=xg_codes[a][:, cols].bitcast(E4M3),
                    lhsT_scale=xg_scales[a][:, cols],
                    rhs=wg[a][:, b * PASS : (b + 1) * PASS].bitcast(E4M3),
                    rhs_scale=first_scales[ROWS * (1 + a) : P, b * PASS : (b + 1) * PASS],
                    start=(a == 0),
                    stop=(a == 1),
                )
            n = PICKS_AT_ONCE + PICKS_AFTER_QUANTISE + unit - FIRST_LENDING_UNIT
            lends = unit >= FIRST_LENDING_UNIT and n < 2 * PACK
            if lends:
                gate = deferred[:, n, :]
            else:
                gate = ring.tile([P, PASS], F32, name="gate", tag="gate", bufs=3)[:]
            nc.scalar.activation(out=in_pair_order(gate), in_=from_r_order(ga[:]), func=TANH)
            ub = bank([P, PASS], ub_tag)
            for a in range(2):
                nc.tensor.matmul_mx(
                    out=ub[:],
                    lhsT=xg_codes[a][:, cols].bitcast(E4M3),
                    lhsT_scale=xg_scales[a][:, cols],
                    rhs=wu[a][:, 2 * b * PASS : 2 * (b + 1) * PASS].bitcast(E2M1),
                    rhs_scale=first_scales[:, a * R + b * PASS : a * R + (b + 1) * PASS],
                    start=(a == 0),
                    stop=(a == 1),
                )
            h_rows[jt, b] = ring.tile([P, PASS], BF16, name="h_rows", tag="h_rows", bufs=6)
            nc.vector.tensor_tensor(
                in_pair_order(h_rows[jt, b][:]), from_r_order(ub[:]), in_pair_order(gate), MULT
            )
            if lends:
                deferred_pick(n)

        h_operand = {}

        def turn(jt, halves, tag):
            count = len(halves)
            turned = bank([P, count, 2, TILE], tag)
            for m, b in enumerate(halves):
                words = h_rows[jt, b][:].bitcast(F32)
                for u in range(2):
                    nc.tensor.transpose(turned[:, m, u, :], words[:, u * P : (u + 1) * P], ident[:])
            h_woven = ring.tile([P, count * TILE * PACK], BF16, name="h_woven", tag="h_woven", bufs=3, align_bytes=64)
            nc.scalar.copy(
                out=h_woven[:].bitcast(F32).rearrange("p (m j u) -> p m j u", m=count, u=2),
                in_=turned[:].rearrange("p m u j -> p m j u"),
            )
            h_codes = ring.tile([P, count * TILE], I32, name="h_codes", tag="h_codes", bufs=4, align_bytes=64)
            h_scales = ring.tile([P, count * TILE], U8, name="h_scales", tag="h_scales", bufs=4, align_bytes=64)
            nc.vector.quantize_mx(out=h_codes[:].bitcast(E4M3), scales=h_scales[:], in_=h_woven[:])
            for m, b in enumerate(halves):
                cols = slice(m * TILE, (m + 1) * TILE)
                h_operand[jt, b] = (h_codes[:, cols], h_scales[:, cols])

        out_codes = keep.tile([P, J], I32, name="out_codes", align_bytes=64)
        out_scales = keep.tile([P, J], U8, name="out_scales", align_bytes=64)
        out_pairs = [keep.tile([P, PACK, PAIR], F32, name="out_%d" % s) for s in range(J // PAIR)]

        def deal_second_weights():
            for dealt, raw in (
                (wd8[:], wd8_raw[:]),
                (wd4[:].bitcast(U16), wd4_raw[:].bitcast(U16)),
                (second_scales[:], second_scales_raw[:]),
            ):
                nc.vector.tensor_copy(
                    out=dealt.rearrange("p (i m) -> p i m", i=PACK),
                    in_=raw.rearrange("p (m i) -> p i m", i=PACK),
                )

        def second_stage(jt, tag):
            y = bank([P, PACK, TILE], tag)
            for b in range(2):
                codes, scales = h_operand[jt, b]
                for i in range(PACK):
                    if b == 0:
                        lhsT = wd8[:, i * P : (i + 1) * P].bitcast(E4M3)
                        lhsT_scale = second_scales[ROWS:P, i * P : (i + 1) * P]
                    else:
                        lhsT = wd4[:, 2 * i * P : 2 * (i + 1) * P].bitcast(E2M1)
                        lhsT_scale = second_scales[:, i * P : (i + 1) * P]
                    nc.tensor.matmul_mx(
                        out=y[:, i, :],
                        lhsT=lhsT,
                        lhsT_scale=lhsT_scale,
                        rhs=codes.bitcast(E4M3),
                        rhs_scale=scales,
                        start=(b == 0 and i == 0),
                        stop=(b == 1 and i == PACK - 1),
                    )
            return y

        def of_tile(pairs, jt):
            s, side = divmod(jt, 2)
            return pairs[s][:, :, side * TILE : (side + 1) * TILE]

        def add_and_store(jt, y):
            nc.vector.tensor_tensor(of_tile(out_pairs, jt), y[:], of_tile(res_pairs, jt), ADD)
            s, side = divmod(jt, 2)
            if jt >= LAST - 1:
                nc.sync.dma_start(out_rows[:, :, jt * TILE : (jt + 1) * TILE], of_tile(out_pairs, jt))
            elif side == 1:
                nc.sync.dma_start(out_rows[:, :, s * PAIR : (s + 1) * PAIR], out_pairs[s][:])

        def hand_on(jt, woven):
            cols = slice(jt * TILE, (jt + 1) * TILE)
            quantise(out_codes[:, cols], out_scales[:, cols], woven)
            if jt % 2 == 1:
                both = slice((jt - 1) * TILE, (jt + 1) * TILE)
                nc.sync.dma_start(out_words[:, both], out_codes[:, both])

        def weave_and_hand_on(jt):
            woven = woven_tile(TILE, "woven_out")[:]
            weave(nc, woven, of_tile(out_pairs, jt))
            hand_on(jt, woven)

        for jt in range(TILES // 2):
            pick(late[:, PACK - 1, jt * TILE : (jt + 1) * TILE], 1, PACK - 1, jt * TILE, (jt + 1) * TILE)
        for jt in range(TILES // 2 - 1):
            quantise_late(jt)

        res_woven = keep.tile([P, TILE, PACK], F32, name="res_woven")
        for step in range(LAST):
            first_stage(step, 0)
            first_stage(step, 1)
            if step == 0:
                quantise_late(TILES // 2 - 1)
            if step == 1:
                deal_second_weights()
            if step >= 1:
                turn(step - 1, (0, 1), "turned")
            if step >= 2:
                add_and_store(step - 2, second_stage(step - 2, "y"))
            if step >= 3:
                weave_and_hand_on(step - 3)
        weave(nc, res_woven[:], of_tile(res_pairs, LAST))

        first_stage(LAST, 0)
        first_stage(LAST, 1)
        turn(LAST - 1, (0, 1), "turned")
        turn(LAST, (0,), "ga")
        turn(LAST, (1,), "ub")
        add_and_store(LAST - 2, second_stage(LAST - 2, "y"))
        add_and_store(LAST - 1, second_stage(LAST - 1, "ga"))
        y_last = second_stage(LAST, "ub")
        for jt in range(LAST - 3, LAST):
            weave_and_hand_on(jt)
        last_woven = keep.tile([P, TILE, PACK], BF16, name="last_woven", align_bytes=64)
        nc.vector.tensor_tensor(last_woven[:], y_last[:].rearrange("p i j -> p j i"), res_woven[:], ADD)
        add_and_store(LAST, y_last)
        hand_on(LAST, last_woven[:])
        for q in range(ROWS):
            nc.scalar.dma_start(
                out_2[0, q:BLOCKS:ROWS, :].bitcast(I32),
                out_scales[q:P:QUADRANT, :].bitcast(I32),
            )
